import numpy as np
import ml_dtypes


def mxq(x, axis, fmt="e4m3"):
    dtype, down = {"e4m3": (ml_dtypes.float8_e4m3fn, 7), "e5m2": (ml_dtypes.float8_e5m2, 14)}[fmt]
    v = np.moveaxis(np.asarray(x, np.float32).astype(ml_dtypes.bfloat16).astype(np.float64), axis, -1)
    blocks = v.reshape(v.shape[:-1] + (-1, 32))
    amax = np.abs(blocks).max(-1, keepdims=True)
    byte = np.maximum(np.where(amax > 0, np.frexp(amax)[1] - 1 + 127, 0) - down, 1)
    scale = np.exp2(byte - 127.0)
    codes = (blocks / scale).astype(np.float32).astype(dtype).astype(np.float64)
    return np.moveaxis((codes * scale).reshape(v.shape), -1, axis)


WIDE = False


def mx_kscale(k):
    if not WIDE:
        return np.ones(k)
    levels = np.array([10, -10, 5, -5, 0])
    if k % 512:
        return np.exp2(np.random.permutation(np.resize(levels, k // 32))).repeat(32)
    a = np.empty((k // 512, 16))
    for p in range(k // 512):
        a[p, :8] = np.random.permutation(np.resize(levels, 8))
        for g in range(8):
            far = levels[np.abs(levels - a[p, g]) >= 10]
            a[p, g + 8] = far[np.random.randint(len(far))]
    return np.exp2(a.ravel()).repeat(32)


def f64(x):
    return np.asarray(x).astype(np.float64)


def striped(idx):
    return np.tile(idx.reshape(-1, 16).T, (8, 1)).astype(np.uint16)


def unstriped(offs):
    return offs[:16].T.reshape(-1).astype(np.int64)


def pack_weight(w):
    k, n = w.shape
    w = f64(np.asarray(w, np.float32).astype(ml_dtypes.bfloat16)).reshape(k // 32, 32, n)
    amax = np.abs(w).max(1)
    byte = np.clip(np.where(amax > 0, np.frexp(amax)[1] - 1 + 127 - 7, 1), 1, 254)
    scaled = (w * np.exp2(127.0 - byte)[:, None, :]).reshape(k, n).astype(np.float32)
    words = np.ascontiguousarray(scaled.reshape(k // 512, 128, 4, n).transpose(0, 1, 3, 2)).astype(ml_dtypes.float8_e4m3fn).view(np.uint8)
    return words, np.ascontiguousarray(byte.astype(np.uint8).reshape(k // 512, 16, n))


def unpack_weight(words, scales):
    g, p, n, _ = words.shape
    vals = np.ascontiguousarray(words).view(ml_dtypes.float8_e4m3fn).astype(np.float64) * np.repeat(np.exp2(scales.astype(np.float64) - 127.0), 8, axis=1)[..., None]
    return vals.transpose(0, 1, 3, 2).reshape(g * 512, n)


K, T, D, S, V, N = 512, 2048, 2, 768, 384, 128


def setup_inputs():
    n = np.random.standard_normal
    s = mx_kscale(K)[:, None]
    words, scales = pack_weight(n((K, N)) / np.sqrt(K) / s)
    return {
        "xT": (n((K, T)) * s).astype(np.float32),
        "w_words": words,
        "w_scales": scales,
        "gate": np.tile(np.random.uniform(0.2, 1.0, (D, 1, V)) / np.sqrt(D), (1, N, 1)).astype(np.float32),
        "offs": striped(np.random.permutation(T)[:S]),
        "pos1": striped(np.random.permutation(S)[:V]),
        "pos2": striped(np.random.permutation(S)[:V]),
    }


def reference(xT, w_words, w_scales, gate, offs, pos1, pos2):
    w = unpack_weight(w_words, w_scales)
    idx = unstriped(offs)
    xq = mxq(f64(xT)[:, idx], 0, "e4m3")
    y = w.T @ xq
    return sum(f64(gate[d]) * y[:, unstriped(p)] for d, p in enumerate((pos1, pos2)))

@@ -1,0 +1,121 @@
+from contextlib import ExitStack
+
+import concourse.mybir as mybir
+
+K, T, D, S, V, N = 512, 2048, 2, 768, 384, 128
+FLOPS = 2 * K * N * S
+
+F32 = mybir.dt.float32
+BF16 = mybir.dt.bfloat16
+I32 = mybir.dt.int32
+U32 = mybir.dt.uint32
+U16 = mybir.dt.uint16
+U8 = mybir.dt.uint8
+FP8X4 = mybir.dt.float8_e4m3fn_x4
+COPY = mybir.ActivationFunctionType.Copy
+MULT = mybir.AluOpType.mult
+ADD = mybir.AluOpType.add
+
+P = 128
+PACK = 4
+STRIPE = 16
+
+
+def tile_picked_sub_lin_none_sub_e_kernel(tc, xT, w_words, w_scales, gate, offs, pos1, pos2, out):
+    nc = tc.nc
+    with ExitStack() as ctx:
+        lists = ctx.enter_context(tc.tile_pool(name="lists", bufs=1))
+        keep = ctx.enter_context(tc.tile_pool(name="keep", bufs=1))
+        psum = ctx.enter_context(tc.psum_pool(name="psum", bufs=1))
+
+        offs_t = lists.tile([P, S // STRIPE], U16, name="offs_t")
+        pos1_t = lists.tile([P, V // STRIPE], U16, name="pos1_t")
+        pos2_t = lists.tile([P, V // STRIPE], U16, name="pos2_t")
+        x = keep.tile([P, PACK, T], F32, name="x")
+        w_codes = keep.tile([P, N], I32, name="w_codes", align_bytes=64)
+        w_plane = keep.tile([P, N], U8, name="w_plane", align_bytes=64)
+        gates = keep.tile([P, D, V], F32, name="gates")
+        picked = keep.tile([P, PACK, S], F32, name="picked")
+        grouped = keep.tile([P, S, PACK], BF16, name="grouped", align_bytes=64)
+        codes = keep.tile([P, S], U32, name="codes", align_bytes=64)
+        scales = keep.tile([P, S], U8, name="scales", align_bytes=64)
+        y = keep.tile([P, S], F32, name="y")
+        term1 = keep.tile([P, V], F32, name="term1")
+        term2 = keep.tile([P, V], F32, name="term2")
+        total = keep.tile([P, V], F32, name="total")
+
+        planes = xT.rearrange("(p t) n -> p t n", t=PACK)
+        nc.sync.dma_start(out=x[:, 0, :], in_=planes[:, 0, :])
+        nc.sync.dma_start(offs_t[:], offs)
+        for t in range(1, PACK):
+            nc.sync.dma_start(out=x[:, t, :], in_=planes[:, t, :])
+        nc.sync.dma_start(out=w_codes[:], in_=w_words[0].rearrange("p n t -> p (n t)").bitcast(I32))
+        nc.vector.memset(w_plane[:].bitcast(I32), 0)
+        for q in range(4):
+            nc.sync.dma_start(
+                out=w_plane[32 * q : 32 * q + 4, :].bitcast(I32),
+                in_=w_scales[0, 4 * q : 4 * q + 4, :].bitcast(I32),
+            )
+        nc.sync.dma_start(out=gates[:], in_=gate.rearrange("d m v -> m d v"))
+        nc.sync.dma_start(pos1_t[:], pos1)
+        nc.sync.dma_start(pos2_t[:], pos2)
+
+
+        def entries(a, b):
+            return offs_t[:, a // STRIPE : b // STRIPE]
+
+        def gather_plain(t, a, b):
+            nc.vector.tensor_copy(picked[:, t, a:b], x[:, t, :].indirect(entries(a, b)))
+
+        def gather_stepped(t, a, b):
+            nc.vector.tensor_copy(grouped[:, a:b, t], x[:, t, :].indirect(entries(a, b)))
+
+        def interleave_pair(t, a, b):
+            nc.scalar.activation(
+                grouped[:, a:b, t : t + 2], picked[:, t : t + 2, a:b].rearrange("p t n -> p n t"), COPY
+            )
+
+        def multiply(a, b):
+            nc.vector.quantize_mx(
+                out=codes[:, a:b].bitcast(FP8X4),
+                scales=scales[:, a:b],
+                in_=grouped[:, a:b, :].rearrange("p n t -> p (n t)"),
+            )
+            acc = psum.tile([P, b - a], F32, name=f"acc{a}")
+            nc.tensor.matmul_mx(
+                out=acc[:],
+                lhsT=w_codes[:].bitcast(FP8X4),
+                lhsT_scale=w_plane[:],
+                rhs=codes[:, a:b].bitcast(FP8X4),
+                rhs_scale=scales[:, a:b],
+                start=True,
+                stop=True,
+            )
+            nc.scalar.activation(y[:, a:b], acc[:], COPY)
+
+        gather_plain(0, 0, S)
+        gather_plain(1, 0, 256)
+        interleave_pair(0, 0, 256)
+        gather_plain(1, 256, S)
+        interleave_pair(0, 256, S)
+        gather_plain(2, 0, 512)
+        gather_stepped(2, 512, S)
+        gather_plain(3, 0, 256)
+        interleave_pair(2, 0, 256)
+        gather_plain(3, 256, 512)
+        interleave_pair(2, 256, 512)
+        gather_stepped(3, 512, S)
+        multiply(0, 256)
+        multiply(512, S)
+        multiply(256, 384)
+        multiply(384, 512)
+
+        nc.vector.tensor_tensor(term1[:], y[:].indirect(pos1_t[:]), gates[:, 0, :], MULT)
+        halves = ((0, 192), (192, V))
+        for a, b in halves:
+            nc.vector.tensor_tensor(
+                term2[:, a:b], y[:].indirect(pos2_t[:, a // STRIPE : b // STRIPE]), gates[:, 1, a:b], MULT
+            )
+        for (a, b), queue in zip(halves, (nc.sync, nc.scalar)):
+            nc.vector.tensor_tensor(total[:, a:b], term1[:, a:b], term2[:, a:b], ADD)
+            queue.dma_start(out=out[:, a:b], in_=total[:, a:b])

@@ -75,7 +75,7 @@ def tile_picked_sub_lin_none_sub_e_kernel(tc, xT, w_words, w_scales, gate, offs,
                 grouped[:, a:b, t : t + 2], picked[:, t : t + 2, a:b].rearrange("p t n -> p n t"), COPY
             )
 
-        def multiply(a, b):
+        def multiply(a, b, on_vector):
             nc.vector.quantize_mx(
                 out=codes[:, a:b].bitcast(FP8X4),
                 scales=scales[:, a:b],
@@ -91,13 +91,16 @@ def tile_picked_sub_lin_none_sub_e_kernel(tc, xT, w_words, w_scales, gate, offs,
                 start=True,
                 stop=True,
             )
-            nc.scalar.activation(y[:, a:b], acc[:], COPY)
+            if on_vector:
+                nc.vector.tensor_copy(y[:, a:b], acc[:])
+            else:
+                nc.scalar.activation(y[:, a:b], acc[:], COPY)
 
         gather_plain(0, 0, S)
-        gather_plain(1, 0, 256)
-        interleave_pair(0, 0, 256)
-        gather_plain(1, 256, S)
-        interleave_pair(0, 256, S)
+        gather_plain(1, 512, S)
+        interleave_pair(0, 512, S)
+        gather_plain(1, 0, 512)
+        interleave_pair(0, 0, 512)
         gather_plain(2, 0, 512)
         gather_stepped(2, 512, S)
         gather_plain(3, 0, 256)
@@ -105,10 +108,10 @@ def tile_picked_sub_lin_none_sub_e_kernel(tc, xT, w_words, w_scales, gate, offs,
         gather_plain(3, 256, 512)
         interleave_pair(2, 256, 512)
         gather_stepped(3, 512, S)
-        multiply(0, 256)
-        multiply(512, S)
-        multiply(256, 384)
-        multiply(384, 512)
+        multiply(0, 256, False)
+        multiply(512, 768, False)
+        multiply(256, 384, True)
+        multiply(384, 512, False)
 
         nc.vector.tensor_tensor(term1[:], y[:].indirect(pos1_t[:]), gates[:, 0, :], MULT)
         halves = ((0, 192), (192, V))

@@ -45,17 +45,18 @@ def tile_picked_sub_lin_none_sub_e_kernel(tc, xT, w_words, w_scales, gate, offs,
         total = keep.tile([P, V], F32, name="total")
 
         planes = xT.rearrange("(p t) n -> p t n", t=PACK)
+        nc.vector.memset(w_plane[:].bitcast(I32), 0)
         nc.sync.dma_start(out=x[:, 0, :], in_=planes[:, 0, :])
         nc.sync.dma_start(offs_t[:], offs)
-        for t in range(1, PACK):
-            nc.sync.dma_start(out=x[:, t, :], in_=planes[:, t, :])
-        nc.sync.dma_start(out=w_codes[:], in_=w_words[0].rearrange("p n t -> p (n t)").bitcast(I32))
-        nc.vector.memset(w_plane[:].bitcast(I32), 0)
+        nc.sync.dma_start(out=x[:, 1, :], in_=planes[:, 1, :])
         for q in range(4):
             nc.sync.dma_start(
                 out=w_plane[32 * q : 32 * q + 4, :].bitcast(I32),
                 in_=w_scales[0, 4 * q : 4 * q + 4, :].bitcast(I32),
             )
+        for t in range(2, PACK):
+            nc.sync.dma_start(out=x[:, t, :], in_=planes[:, t, :])
+        nc.sync.dma_start(out=w_codes[:], in_=w_words[0].rearrange("p n t -> p (n t)").bitcast(I32))
         nc.sync.dma_start(out=gates[:], in_=gate.rearrange("d m v -> m d v"))
         nc.sync.dma_start(pos1_t[:], pos1)
         nc.sync.dma_start(pos2_t[:], pos2)

@@ -19,6 +19,7 @@ ADD = mybir.AluOpType.add
 P = 128
 PACK = 4
 STRIPE = 16
+THIRD = 256
 
 
 def tile_picked_sub_lin_none_sub_e_kernel(tc, xT, w_words, w_scales, gate, offs, pos1, pos2, out):
@@ -35,8 +36,8 @@ def tile_picked_sub_lin_none_sub_e_kernel(tc, xT, w_words, w_scales, gate, offs,
         w_codes = keep.tile([P, N], I32, name="w_codes", align_bytes=64)
         w_plane = keep.tile([P, N], U8, name="w_plane", align_bytes=64)
         gates = keep.tile([P, D, V], F32, name="gates")
-        picked = keep.tile([P, PACK, S], F32, name="picked")
-        grouped = keep.tile([P, S, PACK], BF16, name="grouped", align_bytes=64)
+        picked = keep.tile([P, 2, S], F32, name="picked")
+        pairs = [keep.tile([P, 2, THIRD, 2], BF16, name=f"pairs{i}") for i in range(S // THIRD)]
         codes = keep.tile([P, S], U32, name="codes", align_bytes=64)
         scales = keep.tile([P, S], U8, name="scales", align_bytes=64)
         y = keep.tile([P, S], F32, name="y")
@@ -68,19 +69,29 @@ def tile_picked_sub_lin_none_sub_e_kernel(tc, xT, w_words, w_scales, gate, offs,
         def gather_plain(t, a, b):
             nc.vector.tensor_copy(picked[:, t, a:b], x[:, t, :].indirect(entries(a, b)))
 
-        def gather_stepped(t, a, b):
-            nc.vector.tensor_copy(grouped[:, a:b, t], x[:, t, :].indirect(entries(a, b)))
+        def gather_into_pair(t, i):
+            nc.vector.tensor_copy(
+                pairs[i][:, 1, :, t - 2], x[:, t, :].indirect(entries(i * THIRD, (i + 1) * THIRD))
+            )
 
-        def interleave_pair(t, a, b):
+        def first_pair(i):
             nc.scalar.activation(
-                grouped[:, a:b, t : t + 2], picked[:, t : t + 2, a:b].rearrange("p t n -> p n t"), COPY
+                pairs[i][:, 0, :, :],
+                picked[:, :, i * THIRD : (i + 1) * THIRD].rearrange("p t n -> p n t"),
+                COPY,
             )
 
         def multiply(a, b, on_vector):
+            grouped = keep.tile([P, b - a, PACK], BF16, name=f"grouped{a}", align_bytes=64)
+            i, lo = divmod(a, THIRD)
+            words = pairs[i][:].rearrange("p u n e -> p u (n e)").bitcast(U32)
+            nc.scalar.copy(
+                grouped[:].bitcast(U32), words[:, :, lo : lo + b - a].rearrange("p u n -> p n u")
+            )
             nc.vector.quantize_mx(
                 out=codes[:, a:b].bitcast(FP8X4),
                 scales=scales[:, a:b],
-                in_=grouped[:, a:b, :].rearrange("p n t -> p (n t)"),
+                in_=grouped[:].rearrange("p n t -> p (n t)"),
             )
             acc = psum.tile([P, b - a], F32, name=f"acc{a}")
             nc.tensor.matmul_mx(
@@ -92,27 +103,22 @@ def tile_picked_sub_lin_none_sub_e_kernel(tc, xT, w_words, w_scales, gate, offs,
                 start=True,
                 stop=True,
             )
+            return acc
+
+        gather_plain(0, 0, S)
+        gather_plain(1, 0, S)
+        for i in range(S // THIRD):
+            first_pair(i)
+        for t in (2, 3):
+            for i in range(S // THIRD):
+                gather_into_pair(t, i)
+        pieces = ((0, 256, False), (256, 512, False), (512, 640, True), (640, 768, False))
+        sums = [multiply(a, b, on_vector) for a, b, on_vector in pieces]
+        for (a, b, on_vector), acc in zip(pieces, sums):
             if on_vector:
                 nc.vector.tensor_copy(y[:, a:b], acc[:])
             else:
                 nc.scalar.activation(y[:, a:b], acc[:], COPY)
-
-        gather_plain(0, 0, S)
-        gather_plain(1, 512, S)
-        interleave_pair(0, 512, S)
-        gather_plain(1, 0, 512)
-        interleave_pair(0, 0, 512)
-        gather_plain(2, 0, 512)
-        gather_stepped(2, 512, S)
-        gather_plain(3, 0, 256)
-        interleave_pair(2, 0, 256)
-        gather_plain(3, 256, 512)
-        interleave_pair(2, 256, 512)
-        gather_stepped(3, 512, S)
-        multiply(0, 256, False)
-        multiply(512, 768, False)
-        multiply(256, 384, True)
-        multiply(384, 512, False)
 
         nc.vector.tensor_tensor(term1[:], y[:].indirect(pos1_t[:]), gates[:, 0, :], MULT)
         halves = ((0, 192), (192, V))

@@ -37,8 +37,11 @@ def tile_picked_sub_lin_none_sub_e_kernel(tc, xT, w_words, w_scales, gate, offs,
         w_plane = keep.tile([P, N], U8, name="w_plane", align_bytes=64)
         gates = keep.tile([P, D, V], F32, name="gates")
         picked = keep.tile([P, 2, S], F32, name="picked")
-        pairs = [keep.tile([P, 2, THIRD, 2], BF16, name=f"pairs{i}") for i in range(S // THIRD)]
-        codes = keep.tile([P, S], U32, name="codes", align_bytes=64)
+        pairs = [
+            keep.tile([P, 2, THIRD, 2], BF16, name=f"pairs{i}", tag=f"turn{i}", align_bytes=64)
+            for i in range(S // THIRD)
+        ]
+        codes = keep.tile([P, 640], U32, name="codes", align_bytes=64)
         scales = keep.tile([P, S], U8, name="scales", align_bytes=64)
         y = keep.tile([P, S], F32, name="y")
         term1 = keep.tile([P, V], F32, name="term1")
@@ -81,15 +84,16 @@ def tile_picked_sub_lin_none_sub_e_kernel(tc, xT, w_words, w_scales, gate, offs,
                 COPY,
             )
 
-        def multiply(a, b, on_vector):
-            grouped = keep.tile([P, b - a, PACK], BF16, name=f"grouped{a}", align_bytes=64)
+        def weave(a, b, copy, word, tag):
+            grouped = keep.tile([P, b - a, PACK], BF16, name=f"grouped{a}", tag=tag, align_bytes=64)
             i, lo = divmod(a, THIRD)
-            words = pairs[i][:].rearrange("p u n e -> p u (n e)").bitcast(U32)
-            nc.scalar.copy(
-                grouped[:].bitcast(U32), words[:, :, lo : lo + b - a].rearrange("p u n -> p n u")
-            )
+            words = pairs[i][:].rearrange("p u n e -> p u (n e)").bitcast(word)
+            copy(grouped[:].bitcast(word), words[:, :, lo : lo + b - a].rearrange("p u n -> p n u"))
+            return grouped
+
+        def multiply(a, b, grouped, words):
             nc.vector.quantize_mx(
-                out=codes[:, a:b].bitcast(FP8X4),
+                out=words.bitcast(FP8X4),
                 scales=scales[:, a:b],
                 in_=grouped[:].rearrange("p n t -> p (n t)"),
             )
@@ -98,7 +102,7 @@ def tile_picked_sub_lin_none_sub_e_kernel(tc, xT, w_words, w_scales, gate, offs,
                 out=acc[:],
                 lhsT=w_codes[:].bitcast(FP8X4),
                 lhsT_scale=w_plane[:],
-                rhs=codes[:, a:b].bitcast(FP8X4),
+                rhs=words.bitcast(FP8X4),
                 rhs_scale=scales[:, a:b],
                 start=True,
                 stop=True,
@@ -112,16 +116,25 @@ def tile_picked_sub_lin_none_sub_e_kernel(tc, xT, w_words, w_scales, gate, offs,
         for t in (2, 3):
             for i in range(S // THIRD):
                 gather_into_pair(t, i)
-        pieces = ((0, 256, False), (256, 512, False), (512, 640, True), (640, 768, False))
-        sums = [multiply(a, b, on_vector) for a, b, on_vector in pieces]
-        for (a, b, on_vector), acc in zip(pieces, sums):
-            if on_vector:
-                nc.vector.tensor_copy(y[:, a:b], acc[:])
-            else:
-                nc.scalar.activation(y[:, a:b], acc[:], COPY)
+        group0 = weave(0, 256, nc.scalar.copy, U32, "group0")
+        group1 = weave(256, 384, nc.scalar.copy, U32, "group1")
+        group2 = weave(384, 512, nc.scalar.copy, U32, "group2")
+        group3 = weave(512, 640, nc.scalar.copy, U32, "group3")
+        acc0 = multiply(0, 256, group0, codes[:, 0:256])
+        group4 = weave(640, 768, nc.vector.tensor_copy, I32, "turn0")
+        acc1 = multiply(256, 384, group1, codes[:, 256:384])
+        acc2 = multiply(384, 512, group2, codes[:, 384:512])
+        last_codes = keep.tile([P, 128], U32, name="last_codes", tag="turn1", align_bytes=64)
+        acc4 = multiply(640, 768, group4, last_codes[:])
+        acc3 = multiply(512, 640, group3, codes[:, 512:640])
+        nc.scalar.activation(y[:, 0:256], acc0[:], COPY)
+        nc.scalar.activation(y[:, 256:384], acc1[:], COPY)
+        nc.scalar.activation(y[:, 384:512], acc2[:], COPY)
+        nc.vector.tensor_copy(y[:, 640:768], acc4[:])
+        nc.scalar.activation(y[:, 512:640], acc3[:], COPY)
 
         nc.vector.tensor_tensor(term1[:], y[:].indirect(pos1_t[:]), gates[:, 0, :], MULT)
-        halves = ((0, 192), (192, V))
+        halves = ((0, 256), (256, V))
         for a, b in halves:
             nc.vector.tensor_tensor(
                 term2[:, a:b], y[:].indirect(pos2_t[:, a // STRIPE : b // STRIPE]), gates[:, 1, a:b], MULT

@@ -139,6 +139,6 @@ def tile_picked_sub_lin_none_sub_e_kernel(tc, xT, w_words, w_scales, gate, offs,
             nc.vector.tensor_tensor(
                 term2[:, a:b], y[:].indirect(pos2_t[:, a // STRIPE : b // STRIPE]), gates[:, 1, a:b], MULT
             )
-        for (a, b), queue in zip(halves, (nc.sync, nc.scalar)):
+        for a, b in halves:
             nc.vector.tensor_tensor(total[:, a:b], term1[:, a:b], term2[:, a:b], ADD)
-            queue.dma_start(out=out[:, a:b], in_=total[:, a:b])
+        nc.sync.dma_start(out=out, in_=total[:])

@@ -127,11 +127,11 @@ def tile_picked_sub_lin_none_sub_e_kernel(tc, xT, w_words, w_scales, gate, offs,
         last_codes = keep.tile([P, 128], U32, name="last_codes", tag="turn1", align_bytes=64)
         acc4 = multiply(640, 768, group4, last_codes[:])
         acc3 = multiply(512, 640, group3, codes[:, 512:640])
-        nc.scalar.activation(y[:, 0:256], acc0[:], COPY)
-        nc.scalar.activation(y[:, 256:384], acc1[:], COPY)
-        nc.scalar.activation(y[:, 384:512], acc2[:], COPY)
-        nc.vector.tensor_copy(y[:, 640:768], acc4[:])
-        nc.scalar.activation(y[:, 512:640], acc3[:], COPY)
+        nc.scalar.copy(y[:, 0:256], acc0[:])
+        nc.scalar.copy(y[:, 256:384], acc1[:])
+        nc.scalar.copy(y[:, 384:512], acc2[:])
+        nc.scalar.copy(y[:, 640:768], acc4[:])
+        nc.scalar.copy(y[:, 512:640], acc3[:])
 
         nc.vector.tensor_tensor(term1[:], y[:].indirect(pos1_t[:]), gates[:, 0, :], MULT)
         halves = ((0, 256), (256, V))

@@ -61,7 +61,9 @@ def tile_picked_sub_lin_none_sub_e_kernel(tc, xT, w_words, w_scales, gate, offs,
         for t in range(2, PACK):
             nc.sync.dma_start(out=x[:, t, :], in_=planes[:, t, :])
         nc.sync.dma_start(out=w_codes[:], in_=w_words[0].rearrange("p n t -> p (n t)").bitcast(I32))
-        nc.sync.dma_start(out=gates[:], in_=gate.rearrange("d m v -> m d v"))
+        for d in range(D):
+            for a, b in ((0, 256), (256, V)) if d else ((0, V),):
+                nc.sync.dma_start(out=gates[:, d, a:b], in_=gate[d, :, a:b])
         nc.sync.dma_start(pos1_t[:], pos1)
         nc.sync.dma_start(pos2_t[:], pos2)
 

@@ -12,7 +12,6 @@ U32 = mybir.dt.uint32
 U16 = mybir.dt.uint16
 U8 = mybir.dt.uint8
 FP8X4 = mybir.dt.float8_e4m3fn_x4
-COPY = mybir.ActivationFunctionType.Copy
 MULT = mybir.AluOpType.mult
 ADD = mybir.AluOpType.add
 
@@ -36,7 +35,6 @@ def tile_picked_sub_lin_none_sub_e_kernel(tc, xT, w_words, w_scales, gate, offs,
         w_codes = keep.tile([P, N], I32, name="w_codes", align_bytes=64)
         w_plane = keep.tile([P, N], U8, name="w_plane", align_bytes=64)
         gates = keep.tile([P, D, V], F32, name="gates")
-        picked = keep.tile([P, 2, S], F32, name="picked")
         pairs = [
             keep.tile([P, 2, THIRD, 2], BF16, name=f"pairs{i}", tag=f"turn{i}", align_bytes=64)
             for i in range(S // THIRD)
@@ -71,19 +69,9 @@ def tile_picked_sub_lin_none_sub_e_kernel(tc, xT, w_words, w_scales, gate, offs,
         def entries(a, b):
             return offs_t[:, a // STRIPE : b // STRIPE]
 
-        def gather_plain(t, a, b):
-            nc.vector.tensor_copy(picked[:, t, a:b], x[:, t, :].indirect(entries(a, b)))
-
         def gather_into_pair(t, i):
             nc.vector.tensor_copy(
-                pairs[i][:, 1, :, t - 2], x[:, t, :].indirect(entries(i * THIRD, (i + 1) * THIRD))
-            )
-
-        def first_pair(i):
-            nc.scalar.activation(
-                pairs[i][:, 0, :, :],
-                picked[:, :, i * THIRD : (i + 1) * THIRD].rearrange("p t n -> p n t"),
-                COPY,
+                pairs[i][:, t // 2, :, t % 2], x[:, t, :].indirect(entries(i * THIRD, (i + 1) * THIRD))
             )
 
         def weave(a, b, copy, word, tag):
@@ -111,11 +99,7 @@ def tile_picked_sub_lin_none_sub_e_kernel(tc, xT, w_words, w_scales, gate, offs,
             )
             return acc
 
-        gather_plain(0, 0, S)
-        gather_plain(1, 0, S)
-        for i in range(S // THIRD):
-            first_pair(i)
-        for t in (2, 3):
+        for t in range(PACK):
             for i in range(S // THIRD):
                 gather_into_pair(t, i)
         group0 = weave(0, 256, nc.scalar.copy, U32, "group0")

@@ -31,7 +31,7 @@ def tile_picked_sub_lin_none_sub_e_kernel(tc, xT, w_words, w_scales, gate, offs,
         offs_t = lists.tile([P, S // STRIPE], U16, name="offs_t")
         pos1_t = lists.tile([P, V // STRIPE], U16, name="pos1_t")
         pos2_t = lists.tile([P, V // STRIPE], U16, name="pos2_t")
-        x = keep.tile([P, PACK, T], F32, name="x")
+        x = keep.tile([P, PACK, T], F32, name="x", align_bytes=256)
         w_codes = keep.tile([P, N], I32, name="w_codes", align_bytes=64)
         w_plane = keep.tile([P, N], U8, name="w_plane", align_bytes=64)
         gates = keep.tile([P, D, V], F32, name="gates")
@@ -44,7 +44,7 @@ def tile_picked_sub_lin_none_sub_e_kernel(tc, xT, w_words, w_scales, gate, offs,
         y = keep.tile([P, S], F32, name="y")
         term1 = keep.tile([P, V], F32, name="term1")
         term2 = keep.tile([P, V], F32, name="term2")
-        total = keep.tile([P, V], F32, name="total")
+        total = keep.tile([P, V], F32, name="total", align_bytes=256)
 
         planes = xT.rearrange("(p t) n -> p t n", t=PACK)
         nc.vector.memset(w_plane[:].bitcast(I32), 0)

@@ -50,21 +50,19 @@ def tile_picked_sub_lin_none_sub_e_kernel(tc, xT, w_words, w_scales, gate, offs,
         nc.vector.memset(w_plane[:].bitcast(I32), 0)
         nc.sync.dma_start(out=x[:, 0, :], in_=planes[:, 0, :])
         nc.sync.dma_start(offs_t[:], offs)
-        nc.sync.dma_start(out=x[:, 1, :], in_=planes[:, 1, :])
+        for t in range(1, PACK):
+            nc.sync.dma_start(out=x[:, t, :], in_=planes[:, t, :])
         for q in range(4):
             nc.sync.dma_start(
                 out=w_plane[32 * q : 32 * q + 4, :].bitcast(I32),
                 in_=w_scales[0, 4 * q : 4 * q + 4, :].bitcast(I32),
             )
-        for t in range(2, PACK):
-            nc.sync.dma_start(out=x[:, t, :], in_=planes[:, t, :])
         nc.sync.dma_start(out=w_codes[:], in_=w_words[0].rearrange("p n t -> p (n t)").bitcast(I32))
-        for d in range(D):
-            for a, b in ((0, 256), (256, V)) if d else ((0, V),):
-                nc.sync.dma_start(out=gates[:, d, a:b], in_=gate[d, :, a:b])
+        for a, b in ((0, 256), (256, V)):
+            nc.sync.dma_start(out=gates[:, 0, a:b], in_=gate[0, :, a:b])
         nc.sync.dma_start(pos1_t[:], pos1)
         nc.sync.dma_start(pos2_t[:], pos2)
-
+        nc.sync.dma_start(out=gates[:, 1, :], in_=gate[1])
 
         def entries(a, b):
             return offs_t[:, a // STRIPE : b // STRIPE]
@@ -85,7 +83,7 @@ def tile_picked_sub_lin_none_sub_e_kernel(tc, xT, w_words, w_scales, gate, offs,
             nc.vector.quantize_mx(
                 out=words.bitcast(FP8X4),
                 scales=scales[:, a:b],
-                in_=grouped[:].rearrange("p n t -> p (n t)"),
+                in_=grouped.rearrange("p n t -> p (n t)"),
             )
             acc = psum.tile([P, b - a], F32, name=f"acc{a}")
             nc.tensor.matmul_mx(
@@ -106,14 +104,16 @@ def tile_picked_sub_lin_none_sub_e_kernel(tc, xT, w_words, w_scales, gate, offs,
         group1 = weave(256, 384, nc.scalar.copy, U32, "group1")
         group2 = weave(384, 512, nc.scalar.copy, U32, "group2")
         group3 = weave(512, 640, nc.scalar.copy, U32, "group3")
-        acc0 = multiply(0, 256, group0, codes[:, 0:256])
+        acc0 = multiply(0, 128, group0[:, 0:128, :], codes[:, 0:128])
+        acc0b = multiply(128, 256, group0[:, 128:256, :], codes[:, 128:256])
         group4 = weave(640, 768, nc.vector.tensor_copy, I32, "turn0")
-        acc1 = multiply(256, 384, group1, codes[:, 256:384])
-        acc2 = multiply(384, 512, group2, codes[:, 384:512])
+        acc1 = multiply(256, 384, group1[:], codes[:, 256:384])
+        acc2 = multiply(384, 512, group2[:], codes[:, 384:512])
         last_codes = keep.tile([P, 128], U32, name="last_codes", tag="turn1", align_bytes=64)
-        acc4 = multiply(640, 768, group4, last_codes[:])
-        acc3 = multiply(512, 640, group3, codes[:, 512:640])
-        nc.scalar.copy(y[:, 0:256], acc0[:])
+        acc4 = multiply(640, 768, group4[:], last_codes[:])
+        acc3 = multiply(512, 640, group3[:], codes[:, 512:640])
+        nc.scalar.copy(y[:, 0:128], acc0[:])
+        nc.scalar.copy(y[:, 128:256], acc0b[:])
         nc.scalar.copy(y[:, 256:384], acc1[:])
         nc.scalar.copy(y[:, 384:512], acc2[:])
         nc.scalar.copy(y[:, 640:768], acc4[:])

@@ -14,6 +14,7 @@ U8 = mybir.dt.uint8
 FP8X4 = mybir.dt.float8_e4m3fn_x4
 MULT = mybir.AluOpType.mult
 ADD = mybir.AluOpType.add
+COPY = mybir.ActivationFunctionType.Copy
 
 P = 128
 PACK = 4
@@ -37,9 +38,11 @@ def tile_picked_sub_lin_none_sub_e_kernel(tc, xT, w_words, w_scales, gate, offs,
         gates = keep.tile([P, D, V], F32, name="gates")
         pairs = [
             keep.tile([P, 2, THIRD, 2], BF16, name=f"pairs{i}", tag=f"turn{i}", align_bytes=64)
-            for i in range(S // THIRD)
+            for i in range(2)
         ]
-        codes = keep.tile([P, 640], U32, name="codes", align_bytes=64)
+        direct = keep.tile([P, THIRD, PACK], BF16, name="direct", align_bytes=64)
+        rounded3 = keep.tile([P, T], BF16, name="rounded3", align_bytes=64)
+        codes = keep.tile([P, S], U32, name="codes", align_bytes=64)
         scales = keep.tile([P, S], U8, name="scales", align_bytes=64)
         y = keep.tile([P, S], F32, name="y")
         term1 = keep.tile([P, V], F32, name="term1")
@@ -50,19 +53,19 @@ def tile_picked_sub_lin_none_sub_e_kernel(tc, xT, w_words, w_scales, gate, offs,
         nc.vector.memset(w_plane[:].bitcast(I32), 0)
         nc.sync.dma_start(out=x[:, 0, :], in_=planes[:, 0, :])
         nc.sync.dma_start(offs_t[:], offs)
-        for t in range(1, PACK):
+        for t in range(1, PACK - 1):
             nc.sync.dma_start(out=x[:, t, :], in_=planes[:, t, :])
+        for a, b in ((0, 1024), (1024, 1792), (1792, T)):
+            nc.sync.dma_start(out=x[:, 3, a:b], in_=planes[:, 3, a:b])
         for q in range(4):
             nc.sync.dma_start(
                 out=w_plane[32 * q : 32 * q + 4, :].bitcast(I32),
                 in_=w_scales[0, 4 * q : 4 * q + 4, :].bitcast(I32),
             )
         nc.sync.dma_start(out=w_codes[:], in_=w_words[0].rearrange("p n t -> p (n t)").bitcast(I32))
-        for a, b in ((0, 256), (256, V)):
-            nc.sync.dma_start(out=gates[:, 0, a:b], in_=gate[0, :, a:b])
+        nc.sync.dma_start(out=gates[:], in_=gate.rearrange("d p v -> p d v"))
         nc.sync.dma_start(pos1_t[:], pos1)
         nc.sync.dma_start(pos2_t[:], pos2)
-        nc.sync.dma_start(out=gates[:, 1, :], in_=gate[1])
 
         def entries(a, b):
             return offs_t[:, a // STRIPE : b // STRIPE]
@@ -97,27 +100,30 @@ def tile_picked_sub_lin_none_sub_e_kernel(tc, xT, w_words, w_scales, gate, offs,
             )
             return acc
 
-        for t in range(PACK):
-            for i in range(S // THIRD):
-                gather_into_pair(t, i)
-        group0 = weave(0, 256, nc.scalar.copy, U32, "group0")
-        group1 = weave(256, 384, nc.scalar.copy, U32, "group1")
-        group2 = weave(384, 512, nc.scalar.copy, U32, "group2")
-        group3 = weave(512, 640, nc.scalar.copy, U32, "group3")
-        acc0 = multiply(0, 128, group0[:, 0:128, :], codes[:, 0:128])
-        acc0b = multiply(128, 256, group0[:, 128:256, :], codes[:, 128:256])
-        group4 = weave(640, 768, nc.vector.tensor_copy, I32, "turn0")
-        acc1 = multiply(256, 384, group1[:], codes[:, 256:384])
-        acc2 = multiply(384, 512, group2[:], codes[:, 384:512])
-        last_codes = keep.tile([P, 128], U32, name="last_codes", tag="turn1", align_bytes=64)
-        acc4 = multiply(640, 768, group4[:], last_codes[:])
-        acc3 = multiply(512, 640, group3[:], codes[:, 512:640])
-        nc.scalar.copy(y[:, 0:128], acc0[:])
-        nc.scalar.copy(y[:, 128:256], acc0b[:])
-        nc.scalar.copy(y[:, 256:384], acc1[:])
-        nc.scalar.copy(y[:, 384:512], acc2[:])
-        nc.scalar.copy(y[:, 640:768], acc4[:])
-        nc.scalar.copy(y[:, 512:640], acc3[:])
+        for t in range(PACK - 1):
+            gather_into_pair(t, 0)
+            gather_into_pair(t, 1)
+            nc.vector.tensor_copy(direct[:, :, t], x[:, t, :].indirect(entries(2 * THIRD, S)))
+        for copy, a, b in (
+            (nc.scalar.copy, 0, 512),
+            (nc.gpsimd.tensor_copy, 512, 1024),
+            (nc.vector.tensor_copy, 1024, 1280),
+            (nc.scalar.copy, 1280, 1536),
+            (nc.gpsimd.tensor_copy, 1536, 1792),
+            (nc.scalar.copy, 1792, T),
+        ):
+            copy(rounded3[:, a:b], x[:, 3, a:b])
+        gather_into_pair(3, 0)
+        gather_into_pair(3, 1)
+        nc.scalar.activation(direct[:, :, 3], rounded3[:].indirect(entries(2 * THIRD, S)), COPY)
+        groups = [weave(i * THIRD, (i + 1) * THIRD, nc.vector.tensor_copy, I32, f"group{i}") for i in range(2)]
+        groups.append(direct)
+        products = []
+        for a in range(0, S, 128):
+            i, lo = divmod(a, THIRD)
+            products.append(multiply(a, a + 128, groups[i][:, lo : lo + 128, :], codes[:, a : a + 128]))
+        for i, acc in enumerate(products):
+            nc.scalar.copy(y[:, 128 * i : 128 * i + 128], acc[:])
 
         nc.vector.tensor_tensor(term1[:], y[:].indirect(pos1_t[:]), gates[:, 0, :], MULT)
         halves = ((0, 256), (256, V))

@@ -41,6 +41,7 @@ def tile_picked_sub_lin_none_sub_e_kernel(tc, xT, w_words, w_scales, gate, offs,
             for i in range(2)
         ]
         direct = keep.tile([P, THIRD, PACK], BF16, name="direct", align_bytes=64)
+        picked2 = keep.tile([P, THIRD], F32, name="picked2", align_bytes=64)
         rounded3 = keep.tile([P, T], BF16, name="rounded3", align_bytes=64)
         codes = keep.tile([P, S], U32, name="codes", align_bytes=64)
         scales = keep.tile([P, S], U8, name="scales", align_bytes=64)
@@ -53,19 +54,21 @@ def tile_picked_sub_lin_none_sub_e_kernel(tc, xT, w_words, w_scales, gate, offs,
         nc.vector.memset(w_plane[:].bitcast(I32), 0)
         nc.sync.dma_start(out=x[:, 0, :], in_=planes[:, 0, :])
         nc.sync.dma_start(offs_t[:], offs)
-        for t in range(1, PACK - 1):
-            nc.sync.dma_start(out=x[:, t, :], in_=planes[:, t, :])
-        for a, b in ((0, 1024), (1024, 1792), (1792, T)):
-            nc.sync.dma_start(out=x[:, 3, a:b], in_=planes[:, 3, a:b])
+        nc.sync.dma_start(out=x[:, 1, :], in_=planes[:, 1, :])
+        x_rows = x[:].rearrange("p t n -> p (t n)")
+        hbm_rows = planes.rearrange("p t n -> p (t n)")
+        for a, b in ((2 * T, 3 * T + 256), (3 * T + 256, 3 * T + 1408), (3 * T + 1408, 4 * T)):
+            nc.sync.dma_start(out=x_rows[:, a:b], in_=hbm_rows[:, a:b])
         for q in range(4):
             nc.sync.dma_start(
                 out=w_plane[32 * q : 32 * q + 4, :].bitcast(I32),
                 in_=w_scales[0, 4 * q : 4 * q + 4, :].bitcast(I32),
             )
         nc.sync.dma_start(out=w_codes[:], in_=w_words[0].rearrange("p n t -> p (n t)").bitcast(I32))
-        nc.sync.dma_start(out=gates[:], in_=gate.rearrange("d p v -> p d v"))
+        nc.sync.dma_start(out=gates[:, 0, :], in_=gate[0])
         nc.sync.dma_start(pos1_t[:], pos1)
         nc.sync.dma_start(pos2_t[:], pos2)
+        nc.sync.dma_start(out=gates[:, 1, :], in_=gate[1])
 
         def entries(a, b):
             return offs_t[:, a // STRIPE : b // STRIPE]
@@ -100,17 +103,20 @@ def tile_picked_sub_lin_none_sub_e_kernel(tc, xT, w_words, w_scales, gate, offs,
             )
             return acc
 
-        for t in range(PACK - 1):
+        for t in range(2):
             gather_into_pair(t, 0)
             gather_into_pair(t, 1)
             nc.vector.tensor_copy(direct[:, :, t], x[:, t, :].indirect(entries(2 * THIRD, S)))
+        nc.vector.tensor_copy(picked2[:], x[:, 2, :].indirect(entries(2 * THIRD, S)))
+        gather_into_pair(2, 0)
+        gather_into_pair(2, 1)
+        nc.scalar.copy(direct[:, :, 2], picked2[:])
         for copy, a, b in (
-            (nc.scalar.copy, 0, 512),
-            (nc.gpsimd.tensor_copy, 512, 1024),
-            (nc.vector.tensor_copy, 1024, 1280),
-            (nc.scalar.copy, 1280, 1536),
-            (nc.gpsimd.tensor_copy, 1536, 1792),
-            (nc.scalar.copy, 1792, T),
+            (nc.gpsimd.tensor_copy, 0, 256),
+            (nc.scalar.copy, 256, 896),
+            (nc.gpsimd.tensor_copy, 896, 1408),
+            (nc.scalar.copy, 1408, 1792),
+            (nc.gpsimd.tensor_copy, 1792, T),
         ):
             copy(rounded3[:, a:b], x[:, 3, a:b])
         gather_into_pair(3, 0)

@@ -19,7 +19,12 @@ COPY = mybir.ActivationFunctionType.Copy
 P = 128
 PACK = 4
 STRIPE = 16
+QUADRANT = 32
 THIRD = 256
+PIECE = 128
+LOAD_CUT = 1344
+ROUND_CUTS = (720, 1712)
+SUM_CUT = 256
 
 
 def tile_picked_sub_lin_none_sub_e_kernel(tc, xT, w_words, w_scales, gate, offs, pos1, pos2, out):
@@ -37,10 +42,9 @@ def tile_picked_sub_lin_none_sub_e_kernel(tc, xT, w_words, w_scales, gate, offs,
         w_plane = keep.tile([P, N], U8, name="w_plane", align_bytes=64)
         gates = keep.tile([P, D, V], F32, name="gates")
         pairs = [
-            keep.tile([P, 2, THIRD, 2], BF16, name=f"pairs{i}", tag=f"turn{i}", align_bytes=64)
-            for i in range(2)
+            keep.tile([P, 2, THIRD, 2], BF16, name=f"pairs{i}", tag=f"turn{i}", align_bytes=64) for i in range(2)
         ]
-        direct = keep.tile([P, THIRD, PACK], BF16, name="direct", align_bytes=64)
+        last_groups = keep.tile([P, THIRD, PACK], BF16, name="last_groups", align_bytes=64)
         picked2 = keep.tile([P, THIRD], F32, name="picked2", align_bytes=64)
         rounded3 = keep.tile([P, T], BF16, name="rounded3", align_bytes=64)
         codes = keep.tile([P, S], U32, name="codes", align_bytes=64)
@@ -52,16 +56,16 @@ def tile_picked_sub_lin_none_sub_e_kernel(tc, xT, w_words, w_scales, gate, offs,
 
         planes = xT.rearrange("(p t) n -> p t n", t=PACK)
         nc.vector.memset(w_plane[:].bitcast(I32), 0)
-        nc.sync.dma_start(out=x[:, 0, :], in_=planes[:, 0, :])
+        nc.sync.dma_start(out=x[:, 2, :], in_=planes[:, 2, :])
         nc.sync.dma_start(offs_t[:], offs)
-        nc.sync.dma_start(out=x[:, 1, :], in_=planes[:, 1, :])
-        x_rows = x[:].rearrange("p t n -> p (t n)")
-        hbm_rows = planes.rearrange("p t n -> p (t n)")
-        for a, b in ((2 * T, 3 * T + 256), (3 * T + 256, 3 * T + 1408), (3 * T + 1408, 4 * T)):
-            nc.sync.dma_start(out=x_rows[:, a:b], in_=hbm_rows[:, a:b])
-        for q in range(4):
+        for t in range(2):
+            nc.sync.dma_start(out=x[:, t, :], in_=planes[:, t, :])
+        plane3_loads = ((0, LOAD_CUT), (LOAD_CUT, T))
+        for a, b in plane3_loads:
+            nc.sync.dma_start(out=x[:, 3, a:b], in_=planes[:, 3, a:b])
+        for q in range(P // QUADRANT):
             nc.sync.dma_start(
-                out=w_plane[32 * q : 32 * q + 4, :].bitcast(I32),
+                out=w_plane[QUADRANT * q : QUADRANT * q + 4, :].bitcast(I32),
                 in_=w_scales[0, 4 * q : 4 * q + 4, :].bitcast(I32),
             )
         nc.sync.dma_start(out=w_codes[:], in_=w_words[0].rearrange("p n t -> p (n t)").bitcast(I32))
@@ -70,73 +74,68 @@ def tile_picked_sub_lin_none_sub_e_kernel(tc, xT, w_words, w_scales, gate, offs,
         nc.sync.dma_start(pos2_t[:], pos2)
         nc.sync.dma_start(out=gates[:, 1, :], in_=gate[1])
 
-        def entries(a, b):
-            return offs_t[:, a // STRIPE : b // STRIPE]
+        def third(i):
+            return offs_t[:, i * THIRD // STRIPE : (i + 1) * THIRD // STRIPE]
 
-        def gather_into_pair(t, i):
-            nc.vector.tensor_copy(
-                pairs[i][:, t // 2, :, t % 2], x[:, t, :].indirect(entries(i * THIRD, (i + 1) * THIRD))
-            )
+        def columns(piece):
+            return slice(piece * PIECE, (piece + 1) * PIECE)
 
-        def weave(a, b, copy, word, tag):
-            grouped = keep.tile([P, b - a, PACK], BF16, name=f"grouped{a}", tag=tag, align_bytes=64)
-            i, lo = divmod(a, THIRD)
+        def gather_into_pairs(t):
+            for i in range(2):
+                nc.vector.tensor_copy(pairs[i][:, t // 2, :, t % 2], x[:, t, :].indirect(third(i)))
+
+        def weave(piece, copy, word, tag):
+            grouped = keep.tile([P, PIECE, PACK], BF16, name=f"grouped{piece * PIECE}", tag=tag, align_bytes=64)
+            i, half = divmod(piece, THIRD // PIECE)
             words = pairs[i][:].rearrange("p u n e -> p u (n e)").bitcast(word)
-            copy(grouped[:].bitcast(word), words[:, :, lo : lo + b - a].rearrange("p u n -> p n u"))
-            return grouped
+            copy(grouped[:].bitcast(word), words[:, :, columns(half)].rearrange("p u n -> p n u"))
+            return grouped[:]
 
-        def multiply(a, b, grouped, words):
+        def multiply(piece, grouped):
             nc.vector.quantize_mx(
-                out=words.bitcast(FP8X4),
-                scales=scales[:, a:b],
+                out=codes[:, columns(piece)].bitcast(FP8X4),
+                scales=scales[:, columns(piece)],
                 in_=grouped.rearrange("p n t -> p (n t)"),
             )
-            acc = psum.tile([P, b - a], F32, name=f"acc{a}")
+            acc = psum.tile([P, PIECE], F32, name=f"acc{piece * PIECE}")
             nc.tensor.matmul_mx(
                 out=acc[:],
                 lhsT=w_codes[:].bitcast(FP8X4),
                 lhsT_scale=w_plane[:],
-                rhs=words.bitcast(FP8X4),
-                rhs_scale=scales[:, a:b],
+                rhs=codes[:, columns(piece)].bitcast(FP8X4),
+                rhs_scale=scales[:, columns(piece)],
                 start=True,
                 stop=True,
             )
             return acc
 
+        nc.vector.tensor_copy(picked2[:], x[:, 2, :].indirect(third(2)))
+        nc.scalar.copy(last_groups[:, :, 2], picked2[:])
+        gather_into_pairs(2)
         for t in range(2):
-            gather_into_pair(t, 0)
-            gather_into_pair(t, 1)
-            nc.vector.tensor_copy(direct[:, :, t], x[:, t, :].indirect(entries(2 * THIRD, S)))
-        nc.vector.tensor_copy(picked2[:], x[:, 2, :].indirect(entries(2 * THIRD, S)))
-        gather_into_pair(2, 0)
-        gather_into_pair(2, 1)
-        nc.scalar.copy(direct[:, :, 2], picked2[:])
-        for copy, a, b in (
-            (nc.gpsimd.tensor_copy, 0, 256),
-            (nc.scalar.copy, 256, 896),
-            (nc.gpsimd.tensor_copy, 896, 1408),
-            (nc.scalar.copy, 1408, 1792),
-            (nc.gpsimd.tensor_copy, 1792, T),
-        ):
-            copy(rounded3[:, a:b], x[:, 3, a:b])
-        gather_into_pair(3, 0)
-        gather_into_pair(3, 1)
-        nc.scalar.activation(direct[:, :, 3], rounded3[:].indirect(entries(2 * THIRD, S)), COPY)
-        groups = [weave(i * THIRD, (i + 1) * THIRD, nc.vector.tensor_copy, I32, f"group{i}") for i in range(2)]
-        groups.append(direct)
-        products = []
-        for a in range(0, S, 128):
-            i, lo = divmod(a, THIRD)
-            products.append(multiply(a, a + 128, groups[i][:, lo : lo + 128, :], codes[:, a : a + 128]))
-        for i, acc in enumerate(products):
-            nc.scalar.copy(y[:, 128 * i : 128 * i + 128], acc[:])
+            gather_into_pairs(t)
+            nc.vector.tensor_copy(last_groups[:, :, t], x[:, t, :].indirect(third(2)))
+
+        for (a, b), cut in zip(plane3_loads, ROUND_CUTS):
+            nc.scalar.copy(rounded3[:, a:cut], x[:, 3, a:cut])
+            nc.gpsimd.tensor_copy(rounded3[:, cut:b], x[:, 3, cut:b])
+        gather_into_pairs(3)
+        nc.scalar.activation(last_groups[:, :, 3], rounded3[:].indirect(third(2)), COPY)
+
+        groups = [weave(piece, nc.vector.tensor_copy, I32, f"group{piece * PIECE}") for piece in range(3)]
+        groups.append(weave(3, nc.scalar.copy, U32, "turn0"))
+        groups.extend(last_groups[:, columns(half), :] for half in range(2))
+        order = (0, 1, 2, 4, 5, 3)
+        products = [multiply(piece, groups[piece]) for piece in order]
+        for piece, acc in zip(order, products):
+            nc.scalar.copy(y[:, columns(piece)], acc[:])
 
         nc.vector.tensor_tensor(term1[:], y[:].indirect(pos1_t[:]), gates[:, 0, :], MULT)
-        halves = ((0, 256), (256, V))
-        for a, b in halves:
+        parts = ((0, SUM_CUT), (SUM_CUT, V))
+        for a, b in parts:
             nc.vector.tensor_tensor(
                 term2[:, a:b], y[:].indirect(pos2_t[:, a // STRIPE : b // STRIPE]), gates[:, 1, a:b], MULT
             )
-        for a, b in halves:
+        for a, b in parts:
             nc.vector.tensor_tensor(total[:, a:b], term1[:, a:b], term2[:, a:b], ADD)
         nc.sync.dma_start(out=out, in_=total[:])

@@ -37,7 +37,7 @@ def tile_picked_sub_lin_none_sub_e_kernel(tc, xT, w_words, w_scales, gate, offs,
         offs_t = lists.tile([P, S // STRIPE], U16, name="offs_t")
         pos1_t = lists.tile([P, V // STRIPE], U16, name="pos1_t")
         pos2_t = lists.tile([P, V // STRIPE], U16, name="pos2_t")
-        x = keep.tile([P, PACK, T], F32, name="x", align_bytes=256)
+        x = [keep.tile([P, T], F32, name=f"x{t}", tag=f"plane{t}", align_bytes=256) for t in range(PACK)]
         w_codes = keep.tile([P, N], I32, name="w_codes", align_bytes=64)
         w_plane = keep.tile([P, N], U8, name="w_plane", align_bytes=64)
         gates = keep.tile([P, D, V], F32, name="gates")
@@ -56,13 +56,13 @@ def tile_picked_sub_lin_none_sub_e_kernel(tc, xT, w_words, w_scales, gate, offs,
 
         planes = xT.rearrange("(p t) n -> p t n", t=PACK)
         nc.vector.memset(w_plane[:].bitcast(I32), 0)
-        nc.sync.dma_start(out=x[:, 2, :], in_=planes[:, 2, :])
+        nc.sync.dma_start(out=x[2][:], in_=planes[:, 2, :])
         nc.sync.dma_start(offs_t[:], offs)
         for t in range(2):
-            nc.sync.dma_start(out=x[:, t, :], in_=planes[:, t, :])
+            nc.sync.dma_start(out=x[t][:], in_=planes[:, t, :])
         plane3_loads = ((0, LOAD_CUT), (LOAD_CUT, T))
         for a, b in plane3_loads:
-            nc.sync.dma_start(out=x[:, 3, a:b], in_=planes[:, 3, a:b])
+            nc.sync.dma_start(out=x[3][:, a:b], in_=planes[:, 3, a:b])
         for q in range(P // QUADRANT):
             nc.sync.dma_start(
                 out=w_plane[QUADRANT * q : QUADRANT * q + 4, :].bitcast(I32),
@@ -82,14 +82,13 @@ def tile_picked_sub_lin_none_sub_e_kernel(tc, xT, w_words, w_scales, gate, offs,
 
         def gather_into_pairs(t):
             for i in range(2):
-                nc.vector.tensor_copy(pairs[i][:, t // 2, :, t % 2], x[:, t, :].indirect(third(i)))
+                nc.vector.tensor_copy(pairs[i][:, t // 2, :, t % 2], x[t][:].indirect(third(i)))
 
-        def weave(piece, copy, word, tag):
-            grouped = keep.tile([P, PIECE, PACK], BF16, name=f"grouped{piece * PIECE}", tag=tag, align_bytes=64)
+        def weave(piece, copy, word, grouped):
             i, half = divmod(piece, THIRD // PIECE)
             words = pairs[i][:].rearrange("p u n e -> p u (n e)").bitcast(word)
-            copy(grouped[:].bitcast(word), words[:, :, columns(half)].rearrange("p u n -> p n u"))
-            return grouped[:]
+            copy(grouped.bitcast(word), words[:, :, columns(half)].rearrange("p u n -> p n u"))
+            return grouped
 
         def multiply(piece, grouped):
             nc.vector.quantize_mx(
@@ -109,23 +108,25 @@ def tile_picked_sub_lin_none_sub_e_kernel(tc, xT, w_words, w_scales, gate, offs,
             )
             return acc
 
-        nc.vector.tensor_copy(picked2[:], x[:, 2, :].indirect(third(2)))
+        nc.vector.tensor_copy(picked2[:], x[2][:].indirect(third(2)))
         nc.scalar.copy(last_groups[:, :, 2], picked2[:])
         gather_into_pairs(2)
         for t in range(2):
             gather_into_pairs(t)
-            nc.vector.tensor_copy(last_groups[:, :, t], x[:, t, :].indirect(third(2)))
+            nc.vector.tensor_copy(last_groups[:, :, t], x[t][:].indirect(third(2)))
 
         for (a, b), cut in zip(plane3_loads, ROUND_CUTS):
-            nc.scalar.copy(rounded3[:, a:cut], x[:, 3, a:cut])
-            nc.gpsimd.tensor_copy(rounded3[:, cut:b], x[:, 3, cut:b])
+            nc.scalar.copy(rounded3[:, a:cut], x[3][:, a:cut])
+            nc.gpsimd.tensor_copy(rounded3[:, cut:b], x[3][:, cut:b])
         gather_into_pairs(3)
         nc.scalar.activation(last_groups[:, :, 3], rounded3[:].indirect(third(2)), COPY)
 
-        groups = [weave(piece, nc.vector.tensor_copy, I32, f"group{piece * PIECE}") for piece in range(3)]
-        groups.append(weave(3, nc.scalar.copy, U32, "turn0"))
+        first_groups = keep.tile([P, THIRD, PACK], BF16, name="first_groups", align_bytes=64)
+        groups = [weave(half, nc.vector.tensor_copy, I32, first_groups[:, columns(half), :]) for half in range(2)]
+        middle_groups = keep.tile([P, THIRD, PACK], BF16, name="middle_groups", tag="plane3", align_bytes=256)
+        groups.extend(weave(2 + half, nc.scalar.copy, U32, middle_groups[:, columns(half), :]) for half in range(2))
         groups.extend(last_groups[:, columns(half), :] for half in range(2))
-        order = (0, 1, 2, 4, 5, 3)
+        order = (0, 1, 4, 5, 2, 3)
         products = [multiply(piece, groups[piece]) for piece in order]
         for piece, acc in zip(order, products):
             nc.scalar.copy(y[:, columns(piece)], acc[:])

@@ -23,7 +23,8 @@ QUADRANT = 32
 THIRD = 256
 PIECE = 128
 LOAD_CUT = 1344
-ROUND_CUTS = (720, 1712)
+ROUND_CUTS = (672, 1712)
+VECTOR_WEAVE = 64
 SUM_CUT = 256
 
 
@@ -41,15 +42,14 @@ def tile_picked_sub_lin_none_sub_e_kernel(tc, xT, w_words, w_scales, gate, offs,
         w_codes = keep.tile([P, N], I32, name="w_codes", align_bytes=64)
         w_plane = keep.tile([P, N], U8, name="w_plane", align_bytes=64)
         gates = keep.tile([P, D, V], F32, name="gates")
-        pairs = [
-            keep.tile([P, 2, THIRD, 2], BF16, name=f"pairs{i}", tag=f"turn{i}", align_bytes=64) for i in range(2)
-        ]
+        first_groups = keep.tile([P, THIRD, PACK], BF16, name="first_groups", align_bytes=64)
+        middle_pairs = keep.tile([P, 2, THIRD, 2], BF16, name="middle_pairs", tag="turn", align_bytes=64)
+        last_pairs = keep.tile([P, 2, THIRD, 2], BF16, name="last_pairs", align_bytes=64)
         last_groups = keep.tile([P, THIRD, PACK], BF16, name="last_groups", align_bytes=64)
         picked2 = keep.tile([P, THIRD], F32, name="picked2", align_bytes=64)
         rounded3 = keep.tile([P, T], BF16, name="rounded3", align_bytes=64)
         codes = keep.tile([P, S], U32, name="codes", align_bytes=64)
         scales = keep.tile([P, S], U8, name="scales", align_bytes=64)
-        y = keep.tile([P, S], F32, name="y")
         term1 = keep.tile([P, V], F32, name="term1")
         term2 = keep.tile([P, V], F32, name="term2")
         total = keep.tile([P, V], F32, name="total", align_bytes=256)
@@ -80,15 +80,9 @@ def tile_picked_sub_lin_none_sub_e_kernel(tc, xT, w_words, w_scales, gate, offs,
         def columns(piece):
             return slice(piece * PIECE, (piece + 1) * PIECE)
 
-        def gather_into_pairs(t):
-            for i in range(2):
-                nc.vector.tensor_copy(pairs[i][:, t // 2, :, t % 2], x[t][:].indirect(third(i)))
-
-        def weave(piece, copy, word, grouped):
-            i, half = divmod(piece, THIRD // PIECE)
-            words = pairs[i][:].rearrange("p u n e -> p u (n e)").bitcast(word)
-            copy(grouped.bitcast(word), words[:, :, columns(half)].rearrange("p u n -> p n u"))
-            return grouped
+        def gather_first_two_thirds(t):
+            nc.vector.tensor_copy(first_groups[:, :, t], x[t][:].indirect(third(0)))
+            nc.vector.tensor_copy(middle_pairs[:, t // 2, :, t % 2], x[t][:].indirect(third(1)))
 
         def multiply(piece, grouped):
             nc.vector.quantize_mx(
@@ -109,26 +103,38 @@ def tile_picked_sub_lin_none_sub_e_kernel(tc, xT, w_words, w_scales, gate, offs,
             return acc
 
         nc.vector.tensor_copy(picked2[:], x[2][:].indirect(third(2)))
-        nc.scalar.copy(last_groups[:, :, 2], picked2[:])
-        gather_into_pairs(2)
+        nc.scalar.copy(last_pairs[:, 1, :, :], picked2[:].unsqueeze(2).to_broadcast([P, THIRD, 2]))
+        gather_first_two_thirds(2)
         for t in range(2):
-            gather_into_pairs(t)
-            nc.vector.tensor_copy(last_groups[:, :, t], x[t][:].indirect(third(2)))
+            nc.vector.tensor_copy(last_pairs[:, 0, :, t], x[t][:].indirect(third(2)))
+            gather_first_two_thirds(t)
+        nc.scalar.copy(
+            last_groups[:].bitcast(U32),
+            last_pairs[:].rearrange("p u n e -> p u (n e)").bitcast(U32).rearrange("p u n -> p n u"),
+        )
 
         for (a, b), cut in zip(plane3_loads, ROUND_CUTS):
             nc.scalar.copy(rounded3[:, a:cut], x[3][:, a:cut])
             nc.gpsimd.tensor_copy(rounded3[:, cut:b], x[3][:, cut:b])
-        gather_into_pairs(3)
+        gather_first_two_thirds(3)
         nc.scalar.activation(last_groups[:, :, 3], rounded3[:].indirect(third(2)), COPY)
 
-        first_groups = keep.tile([P, THIRD, PACK], BF16, name="first_groups", align_bytes=64)
-        groups = [weave(half, nc.vector.tensor_copy, I32, first_groups[:, columns(half), :]) for half in range(2)]
         middle_groups = keep.tile([P, THIRD, PACK], BF16, name="middle_groups", tag="plane3", align_bytes=256)
-        groups.extend(weave(2 + half, nc.scalar.copy, U32, middle_groups[:, columns(half), :]) for half in range(2))
-        groups.extend(last_groups[:, columns(half), :] for half in range(2))
-        order = (0, 1, 4, 5, 2, 3)
-        products = [multiply(piece, groups[piece]) for piece in order]
-        for piece, acc in zip(order, products):
+
+        def weave(a, b, copy, word):
+            words = middle_pairs[:].rearrange("p u n e -> p u (n e)").bitcast(word)
+            copy(middle_groups[:, a:b, :].bitcast(word), words[:, :, a:b].rearrange("p u n -> p n u"))
+
+        products = {piece: multiply(piece, first_groups[:, columns(piece), :]) for piece in range(2)}
+        weave(THIRD - VECTOR_WEAVE, THIRD, nc.vector.tensor_copy, I32)
+        weave(0, PIECE, nc.scalar.copy, U32)
+        weave(PIECE, THIRD - VECTOR_WEAVE, nc.scalar.copy, U32)
+        for half in range(2):
+            products[4 + half] = multiply(4 + half, last_groups[:, columns(half), :])
+        for half in range(2):
+            products[2 + half] = multiply(2 + half, middle_groups[:, columns(half), :])
+        y = keep.tile([P, S], F32, name="y", tag="turn", align_bytes=64)
+        for piece, acc in products.items():
             nc.scalar.copy(y[:, columns(piece)], acc[:])
 
         nc.vector.tensor_tensor(term1[:], y[:].indirect(pos1_t[:]), gates[:, 0, :], MULT)

@@ -24,7 +24,7 @@ THIRD = 256
 PIECE = 128
 LOAD_CUT = 1344
 ROUND_CUTS = (672, 1712)
-VECTOR_WEAVE = 64
+EARLY = 160
 SUM_CUT = 256
 
 
@@ -42,11 +42,14 @@ def tile_picked_sub_lin_none_sub_e_kernel(tc, xT, w_words, w_scales, gate, offs,
         w_codes = keep.tile([P, N], I32, name="w_codes", align_bytes=64)
         w_plane = keep.tile([P, N], U8, name="w_plane", align_bytes=64)
         gates = keep.tile([P, D, V], F32, name="gates")
-        first_groups = keep.tile([P, THIRD, PACK], BF16, name="first_groups", align_bytes=64)
-        middle_pairs = keep.tile([P, 2, THIRD, 2], BF16, name="middle_pairs", tag="turn", align_bytes=64)
-        last_pairs = keep.tile([P, 2, THIRD, 2], BF16, name="last_pairs", align_bytes=64)
-        last_groups = keep.tile([P, THIRD, PACK], BF16, name="last_groups", align_bytes=64)
-        picked2 = keep.tile([P, THIRD], F32, name="picked2", align_bytes=64)
+        low_row = keep.tile([P, S + THIRD], I32, name="low_row", align_bytes=64)
+        low_words = low_row[:].bitcast(U32)
+        low_pairs = low_row[:].bitcast(BF16).rearrange("p (n e) -> p n e", e=2)
+        early_high = keep.tile([P, 2 * EARLY], BF16, name="early_high", tag="turn", align_bytes=64)
+        late_high = keep.tile([P, 2 * (THIRD - EARLY)], BF16, name="late_high", align_bytes=64)
+        rows = [keep.tile([P, THIRD * PACK], BF16, name=f"groups{i}", align_bytes=64) for i in range(3)]
+        groups = [row[:].rearrange("p (n t) -> p n t", t=PACK) for row in rows]
+        group_words = [row[:].bitcast(U32).rearrange("p (n u) -> p n u", u=2) for row in rows]
         rounded3 = keep.tile([P, T], BF16, name="rounded3", align_bytes=64)
         codes = keep.tile([P, S], U32, name="codes", align_bytes=64)
         scales = keep.tile([P, S], U8, name="scales", align_bytes=64)
@@ -56,9 +59,10 @@ def tile_picked_sub_lin_none_sub_e_kernel(tc, xT, w_words, w_scales, gate, offs,
 
         planes = xT.rearrange("(p t) n -> p t n", t=PACK)
         nc.vector.memset(w_plane[:].bitcast(I32), 0)
-        nc.sync.dma_start(out=x[2][:], in_=planes[:, 2, :])
+        nc.vector.memset(low_row[:, S:], 0)
+        nc.sync.dma_start(out=x[0][:], in_=planes[:, 0, :])
         nc.sync.dma_start(offs_t[:], offs)
-        for t in range(2):
+        for t in (1, 2):
             nc.sync.dma_start(out=x[t][:], in_=planes[:, t, :])
         plane3_loads = ((0, LOAD_CUT), (LOAD_CUT, T))
         for a, b in plane3_loads:
@@ -74,66 +78,65 @@ def tile_picked_sub_lin_none_sub_e_kernel(tc, xT, w_words, w_scales, gate, offs,
         nc.sync.dma_start(pos2_t[:], pos2)
         nc.sync.dma_start(out=gates[:, 1, :], in_=gate[1])
 
-        def third(i):
-            return offs_t[:, i * THIRD // STRIPE : (i + 1) * THIRD // STRIPE]
+        def entries(a, b):
+            return offs_t[:, a // STRIPE : b // STRIPE]
 
         def columns(piece):
             return slice(piece * PIECE, (piece + 1) * PIECE)
 
-        def gather_first_two_thirds(t):
-            nc.vector.tensor_copy(first_groups[:, :, t], x[t][:].indirect(third(0)))
-            nc.vector.tensor_copy(middle_pairs[:, t // 2, :, t % 2], x[t][:].indirect(third(1)))
-
-        def multiply(piece, grouped):
+        def multiply(piece, words):
+            third, half = divmod(piece, 2)
             nc.vector.quantize_mx(
-                out=codes[:, columns(piece)].bitcast(FP8X4),
+                out=words.bitcast(FP8X4),
                 scales=scales[:, columns(piece)],
-                in_=grouped.rearrange("p n t -> p (n t)"),
+                in_=rows[third][:, half * PIECE * PACK : (half + 1) * PIECE * PACK],
             )
             acc = psum.tile([P, PIECE], F32, name=f"acc{piece * PIECE}")
             nc.tensor.matmul_mx(
                 out=acc[:],
                 lhsT=w_codes[:].bitcast(FP8X4),
                 lhsT_scale=w_plane[:],
-                rhs=codes[:, columns(piece)].bitcast(FP8X4),
+                rhs=words.bitcast(FP8X4),
                 rhs_scale=scales[:, columns(piece)],
                 start=True,
                 stop=True,
             )
             return acc
 
-        nc.vector.tensor_copy(picked2[:], x[2][:].indirect(third(2)))
-        nc.scalar.copy(last_pairs[:, 1, :, :], picked2[:].unsqueeze(2).to_broadcast([P, THIRD, 2]))
-        gather_first_two_thirds(2)
+        def half_of(high, t):
+            n = high.shape[1] // 2
+            return high[:, (t - 2) * n : (t - 1) * n]
+
+        def place(copy, high, a, b):
+            copy(groups[0][:, a:b, 2:], high[:].rearrange("p (t n) -> p n t", t=2))
+
         for t in range(2):
-            nc.vector.tensor_copy(last_pairs[:, 0, :, t], x[t][:].indirect(third(2)))
-            gather_first_two_thirds(t)
-        nc.scalar.copy(
-            last_groups[:].bitcast(U32),
-            last_pairs[:].rearrange("p u n e -> p u (n e)").bitcast(U32).rearrange("p u n -> p n u"),
-        )
+            nc.vector.tensor_copy(low_pairs[:, :S, t], x[t][:].indirect(offs_t[:]))
+        nc.gpsimd.tensor_copy(group_words[0][:, :, 0], low_words[:, :THIRD])
+        nc.scalar.copy(group_words[1][:, :, 0], low_words[:, THIRD : 2 * THIRD])
+
+        nc.vector.tensor_copy(low_pairs[:, S:, 0], x[2][:].indirect(entries(2 * THIRD, S)))
+        nc.scalar.copy(group_words[2], low_words[:, 2 * THIRD :].rearrange("p (u n) -> p n u", u=2))
+        nc.vector.tensor_copy(half_of(early_high, 2), x[2][:].indirect(entries(0, EARLY)))
+        nc.vector.tensor_copy(half_of(late_high, 2), x[2][:].indirect(entries(EARLY, THIRD)))
+        nc.vector.tensor_copy(groups[1][:, :, 2], x[2][:].indirect(entries(THIRD, 2 * THIRD)))
 
         for (a, b), cut in zip(plane3_loads, ROUND_CUTS):
             nc.scalar.copy(rounded3[:, a:cut], x[3][:, a:cut])
             nc.gpsimd.tensor_copy(rounded3[:, cut:b], x[3][:, cut:b])
-        gather_first_two_thirds(3)
-        nc.scalar.activation(last_groups[:, :, 3], rounded3[:].indirect(third(2)), COPY)
+        nc.vector.tensor_copy(half_of(early_high, 3), x[3][:].indirect(entries(0, EARLY)))
+        nc.vector.tensor_copy(groups[1][:, :, 3], x[3][:].indirect(entries(THIRD, 2 * THIRD)))
+        nc.vector.tensor_copy(half_of(late_high, 3), rounded3[:].indirect(entries(EARLY, THIRD)))
+        nc.scalar.activation(groups[2][:, :, 3], rounded3[:].indirect(entries(2 * THIRD, S)), COPY)
+        place(nc.gpsimd.tensor_copy, early_high, 0, EARLY)
+        place(nc.scalar.copy, late_high, EARLY, THIRD)
 
-        middle_groups = keep.tile([P, THIRD, PACK], BF16, name="middle_groups", tag="plane3", align_bytes=256)
-
-        def weave(a, b, copy, word):
-            words = middle_pairs[:].rearrange("p u n e -> p u (n e)").bitcast(word)
-            copy(middle_groups[:, a:b, :].bitcast(word), words[:, :, a:b].rearrange("p u n -> p n u"))
-
-        products = {piece: multiply(piece, first_groups[:, columns(piece), :]) for piece in range(2)}
-        weave(THIRD - VECTOR_WEAVE, THIRD, nc.vector.tensor_copy, I32)
-        weave(0, PIECE, nc.scalar.copy, U32)
-        weave(PIECE, THIRD - VECTOR_WEAVE, nc.scalar.copy, U32)
-        for half in range(2):
-            products[4 + half] = multiply(4 + half, last_groups[:, columns(half), :])
-        for half in range(2):
-            products[2 + half] = multiply(2 + half, middle_groups[:, columns(half), :])
-        y = keep.tile([P, S], F32, name="y", tag="turn", align_bytes=64)
+        middle_codes = keep.tile([P, THIRD], U32, name="middle_codes", tag="turn", align_bytes=64)
+        products = {}
+        for piece in (0, 2, 3, 4, 5, 1):
+            words = middle_codes[:, columns(piece - 2)] if piece in (2, 3) else codes[:, columns(piece)]
+            products[piece] = multiply(piece, words)
+        y = keep.tile([P, S], F32, name="y", align_bytes=64)
         for piece, acc in products.items():
             nc.scalar.copy(y[:, columns(piece)], acc[:])
 

@@ -22,8 +22,8 @@ STRIPE = 16
 QUADRANT = 32
 THIRD = 256
 PIECE = 128
-LOAD_CUT = 1344
-ROUND_CUTS = (672, 1712)
+LOAD_CUT = 1280
+ROUND_CUTS = (592, 1664)
 EARLY = 160
 SUM_CUT = 256
 
@@ -59,19 +59,24 @@ def tile_picked_sub_lin_none_sub_e_kernel(tc, xT, w_words, w_scales, gate, offs,
 
         planes = xT.rearrange("(p t) n -> p t n", t=PACK)
         nc.vector.memset(w_plane[:].bitcast(I32), 0)
-        nc.vector.memset(low_row[:, S:], 0)
+        nc.vector.memset(low_pairs[:, S:, 1], 0.0)
         nc.sync.dma_start(out=x[0][:], in_=planes[:, 0, :])
         nc.sync.dma_start(offs_t[:], offs)
+
+        def load_scale_rows(q):
+            nc.sync.dma_start(
+                out=w_plane[QUADRANT * q : QUADRANT * q + 4, :].bitcast(I32),
+                in_=w_scales[0, 4 * q : 4 * q + 4, :].bitcast(I32),
+            )
+
+        for q in range(3):
+            load_scale_rows(q)
         for t in (1, 2):
             nc.sync.dma_start(out=x[t][:], in_=planes[:, t, :])
         plane3_loads = ((0, LOAD_CUT), (LOAD_CUT, T))
         for a, b in plane3_loads:
             nc.sync.dma_start(out=x[3][:, a:b], in_=planes[:, 3, a:b])
-        for q in range(P // QUADRANT):
-            nc.sync.dma_start(
-                out=w_plane[QUADRANT * q : QUADRANT * q + 4, :].bitcast(I32),
-                in_=w_scales[0, 4 * q : 4 * q + 4, :].bitcast(I32),
-            )
+        load_scale_rows(3)
         nc.sync.dma_start(out=w_codes[:], in_=w_words[0].rearrange("p n t -> p (n t)").bitcast(I32))
         nc.sync.dma_start(out=gates[:, 0, :], in_=gate[0])
         nc.sync.dma_start(pos1_t[:], pos1)

@@ -69,10 +69,10 @@ def tile_picked_sub_lin_none_sub_e_kernel(tc, xT, w_words, w_scales, gate, offs,
                 in_=w_scales[0, 4 * q : 4 * q + 4, :].bitcast(I32),
             )
 
-        for q in range(3):
-            load_scale_rows(q)
         for t in (1, 2):
             nc.sync.dma_start(out=x[t][:], in_=planes[:, t, :])
+        for q in range(3):
+            load_scale_rows(q)
         plane3_loads = ((0, LOAD_CUT), (LOAD_CUT, T))
         for a, b in plane3_loads:
             nc.sync.dma_start(out=x[3][:, a:b], in_=planes[:, 3, a:b])

@@ -20,12 +20,11 @@ P = 128
 PACK = 4
 STRIPE = 16
 QUADRANT = 32
-THIRD = 256
 PIECE = 128
-LOAD_CUT = 1280
-ROUND_CUTS = (592, 1664)
-EARLY = 160
-SUM_CUT = 256
+GPSIMD_SHARES = ((0, 128), (128, 192))
+VECTOR_SHARE = (192, 544)
+SCALAR_SHARES = ((544, 640), (640, 768))
+HALVES = ((0, 192), (192, 384))
 
 
 def tile_picked_sub_lin_none_sub_e_kernel(tc, xT, w_words, w_scales, gate, offs, pos1, pos2, out):
@@ -38,65 +37,67 @@ def tile_picked_sub_lin_none_sub_e_kernel(tc, xT, w_words, w_scales, gate, offs,
         offs_t = lists.tile([P, S // STRIPE], U16, name="offs_t")
         pos1_t = lists.tile([P, V // STRIPE], U16, name="pos1_t")
         pos2_t = lists.tile([P, V // STRIPE], U16, name="pos2_t")
-        x = [keep.tile([P, T], F32, name=f"x{t}", tag=f"plane{t}", align_bytes=256) for t in range(PACK)]
+        x = [keep.tile([P, T], F32, name=f"x{t}", align_bytes=256) for t in range(PACK)]
         w_codes = keep.tile([P, N], I32, name="w_codes", align_bytes=64)
         w_plane = keep.tile([P, N], U8, name="w_plane", align_bytes=64)
-        gates = keep.tile([P, D, V], F32, name="gates")
-        low_row = keep.tile([P, S + THIRD], I32, name="low_row", align_bytes=64)
+        gate1 = keep.tile([P, V], F32, name="gate1")
+        gate2 = [keep.tile([P, b - a], F32, name=f"gate2_{a}") for a, b in HALVES]
+        low_row = keep.tile([P, S], I32, name="low_row", align_bytes=64)
         low_words = low_row[:].bitcast(U32)
         low_pairs = low_row[:].bitcast(BF16).rearrange("p (n e) -> p n e", e=2)
-        early_high = keep.tile([P, 2 * EARLY], BF16, name="early_high", tag="turn", align_bytes=64)
-        late_high = keep.tile([P, 2 * (THIRD - EARLY)], BF16, name="late_high", align_bytes=64)
-        rows = [keep.tile([P, THIRD * PACK], BF16, name=f"groups{i}", align_bytes=64) for i in range(3)]
-        groups = [row[:].rearrange("p (n t) -> p n t", t=PACK) for row in rows]
-        group_words = [row[:].bitcast(U32).rearrange("p (n u) -> p n u", u=2) for row in rows]
-        rounded3 = keep.tile([P, T], BF16, name="rounded3", align_bytes=64)
+        shares = GPSIMD_SHARES + SCALAR_SHARES
+        high = {
+            a: keep.tile([P, 2 * (b - a)], BF16, name=f"high{a}", tag="turn" if a == 0 else f"high{a}", align_bytes=64)
+            for a, b in shares
+        }
+        row = keep.tile([P, S * PACK], BF16, name="row", align_bytes=64)
+        groups = row[:].rearrange("p (n t) -> p n t", t=PACK)
+        group_words = row[:].bitcast(U32).rearrange("p (n u) -> p n u", u=2)
         codes = keep.tile([P, S], U32, name="codes", align_bytes=64)
         scales = keep.tile([P, S], U8, name="scales", align_bytes=64)
         term1 = keep.tile([P, V], F32, name="term1")
+        picked2 = keep.tile([P, V], F32, name="picked2")
         term2 = keep.tile([P, V], F32, name="term2")
         total = keep.tile([P, V], F32, name="total", align_bytes=256)
 
         planes = xT.rearrange("(p t) n -> p t n", t=PACK)
         nc.vector.memset(w_plane[:].bitcast(I32), 0)
-        nc.vector.memset(low_pairs[:, S:, 1], 0.0)
         nc.sync.dma_start(out=x[0][:], in_=planes[:, 0, :])
         nc.sync.dma_start(offs_t[:], offs)
-
-        def load_scale_rows(q):
+        for t in (1, 2, 3):
+            nc.sync.dma_start(out=x[t][:], in_=planes[:, t, :])
+        for q in range(4):
             nc.sync.dma_start(
                 out=w_plane[QUADRANT * q : QUADRANT * q + 4, :].bitcast(I32),
                 in_=w_scales[0, 4 * q : 4 * q + 4, :].bitcast(I32),
             )
-
-        for t in (1, 2):
-            nc.sync.dma_start(out=x[t][:], in_=planes[:, t, :])
-        for q in range(3):
-            load_scale_rows(q)
-        plane3_loads = ((0, LOAD_CUT), (LOAD_CUT, T))
-        for a, b in plane3_loads:
-            nc.sync.dma_start(out=x[3][:, a:b], in_=planes[:, 3, a:b])
-        load_scale_rows(3)
         nc.sync.dma_start(out=w_codes[:], in_=w_words[0].rearrange("p n t -> p (n t)").bitcast(I32))
-        nc.sync.dma_start(out=gates[:, 0, :], in_=gate[0])
+        nc.sync.dma_start(out=gate1[:], in_=gate[0])
+        nc.sync.dma_start(out=gate2[0][:], in_=gate[1, :, HALVES[0][0] : HALVES[0][1]])
         nc.sync.dma_start(pos1_t[:], pos1)
         nc.sync.dma_start(pos2_t[:], pos2)
-        nc.sync.dma_start(out=gates[:, 1, :], in_=gate[1])
+        nc.sync.dma_start(out=gate2[1][:], in_=gate[1, :, HALVES[1][0] : HALVES[1][1]])
 
-        def entries(a, b):
-            return offs_t[:, a // STRIPE : b // STRIPE]
+        def entries(share):
+            return offs_t[:, share[0] // STRIPE : share[1] // STRIPE]
 
         def columns(piece):
             return slice(piece * PIECE, (piece + 1) * PIECE)
 
+        def high_row(share, t):
+            n = share[1] - share[0]
+            return high[share[0]][:, (t - 2) * n : (t - 1) * n]
+
+        def place(copy, share):
+            copy(groups[:, share[0] : share[1], 2:], high[share[0]][:].rearrange("p (t n) -> p n t", t=2))
+
         def multiply(piece, words):
-            third, half = divmod(piece, 2)
             nc.vector.quantize_mx(
                 out=words.bitcast(FP8X4),
                 scales=scales[:, columns(piece)],
-                in_=rows[third][:, half * PIECE * PACK : (half + 1) * PIECE * PACK],
+                in_=row[:, piece * PIECE * PACK : (piece + 1) * PIECE * PACK],
             )
-            acc = psum.tile([P, PIECE], F32, name=f"acc{piece * PIECE}")
+            acc = psum.tile([P, PIECE], F32, name=f"acc{piece}")
             nc.tensor.matmul_mx(
                 out=acc[:],
                 lhsT=w_codes[:].bitcast(FP8X4),
@@ -108,49 +109,41 @@ def tile_picked_sub_lin_none_sub_e_kernel(tc, xT, w_words, w_scales, gate, offs,
             )
             return acc
 
-        def half_of(high, t):
-            n = high.shape[1] // 2
-            return high[:, (t - 2) * n : (t - 1) * n]
-
-        def place(copy, high, a, b):
-            copy(groups[0][:, a:b, 2:], high[:].rearrange("p (t n) -> p n t", t=2))
-
         for t in range(2):
-            nc.vector.tensor_copy(low_pairs[:, :S, t], x[t][:].indirect(offs_t[:]))
-        nc.gpsimd.tensor_copy(group_words[0][:, :, 0], low_words[:, :THIRD])
-        nc.scalar.copy(group_words[1][:, :, 0], low_words[:, THIRD : 2 * THIRD])
+            nc.vector.tensor_copy(low_pairs[:, :, t], x[t][:].indirect(offs_t[:]))
+        a, b = VECTOR_SHARE
+        nc.scalar.copy(group_words[:, a:b, 0], low_words[:, a:b])
+        nc.gpsimd.tensor_copy(group_words[:, :a, 0], low_words[:, :a])
+        nc.gpsimd.tensor_copy(group_words[:, b:, 0], low_words[:, b:])
 
-        nc.vector.tensor_copy(low_pairs[:, S:, 0], x[2][:].indirect(entries(2 * THIRD, S)))
-        nc.scalar.copy(group_words[2], low_words[:, 2 * THIRD :].rearrange("p (u n) -> p n u", u=2))
-        nc.vector.tensor_copy(half_of(early_high, 2), x[2][:].indirect(entries(0, EARLY)))
-        nc.vector.tensor_copy(half_of(late_high, 2), x[2][:].indirect(entries(EARLY, THIRD)))
-        nc.vector.tensor_copy(groups[1][:, :, 2], x[2][:].indirect(entries(THIRD, 2 * THIRD)))
+        nc.vector.tensor_copy(groups[:, a:b, 2], x[2][:].indirect(entries(VECTOR_SHARE)))
+        for share in SCALAR_SHARES:
+            nc.vector.tensor_copy(high_row(share, 2), x[2][:].indirect(entries(share)))
+        for share in GPSIMD_SHARES:
+            nc.scalar.activation(high_row(share, 2), x[2][:].indirect(entries(share)), COPY)
 
-        for (a, b), cut in zip(plane3_loads, ROUND_CUTS):
-            nc.scalar.copy(rounded3[:, a:cut], x[3][:, a:cut])
-            nc.gpsimd.tensor_copy(rounded3[:, cut:b], x[3][:, cut:b])
-        nc.vector.tensor_copy(half_of(early_high, 3), x[3][:].indirect(entries(0, EARLY)))
-        nc.vector.tensor_copy(groups[1][:, :, 3], x[3][:].indirect(entries(THIRD, 2 * THIRD)))
-        nc.vector.tensor_copy(half_of(late_high, 3), rounded3[:].indirect(entries(EARLY, THIRD)))
-        nc.scalar.activation(groups[2][:, :, 3], rounded3[:].indirect(entries(2 * THIRD, S)), COPY)
-        place(nc.gpsimd.tensor_copy, early_high, 0, EARLY)
-        place(nc.scalar.copy, late_high, EARLY, THIRD)
+        nc.vector.tensor_copy(groups[:, a:b, 3], x[3][:].indirect(entries(VECTOR_SHARE)))
+        for share in shares:
+            nc.scalar.activation(high_row(share, 3), x[3][:].indirect(entries(share)), COPY)
+        for share in GPSIMD_SHARES:
+            place(nc.gpsimd.tensor_copy, share)
+        for share in SCALAR_SHARES:
+            place(nc.scalar.copy, share)
 
-        middle_codes = keep.tile([P, THIRD], U32, name="middle_codes", tag="turn", align_bytes=64)
+        middle_codes = keep.tile([P, 2 * PIECE], U32, name="middle_codes", tag="turn", align_bytes=64)
         products = {}
-        for piece in (0, 2, 3, 4, 5, 1):
+        for piece in (0, 2, 3, 1, 4, 5):
             words = middle_codes[:, columns(piece - 2)] if piece in (2, 3) else codes[:, columns(piece)]
             products[piece] = multiply(piece, words)
         y = keep.tile([P, S], F32, name="y", align_bytes=64)
         for piece, acc in products.items():
             nc.scalar.copy(y[:, columns(piece)], acc[:])
 
-        nc.vector.tensor_tensor(term1[:], y[:].indirect(pos1_t[:]), gates[:, 0, :], MULT)
-        parts = ((0, SUM_CUT), (SUM_CUT, V))
-        for a, b in parts:
-            nc.vector.tensor_tensor(
-                term2[:, a:b], y[:].indirect(pos2_t[:, a // STRIPE : b // STRIPE]), gates[:, 1, a:b], MULT
-            )
-        for a, b in parts:
+        nc.vector.tensor_tensor(term1[:], y[:].indirect(pos1_t[:]), gate1[:], MULT)
+        for a, b in HALVES:
+            nc.scalar.activation(picked2[:, a:b], y[:].indirect(pos2_t[:, a // STRIPE : b // STRIPE]), COPY)
+        for (a, b), weights in zip(HALVES, gate2):
+            nc.vector.tensor_tensor(term2[:, a:b], picked2[:, a:b], weights[:], MULT)
+        for a, b in HALVES:
             nc.vector.tensor_tensor(total[:, a:b], term1[:, a:b], term2[:, a:b], ADD)
         nc.sync.dma_start(out=out, in_=total[:])

@@ -25,6 +25,7 @@ GPSIMD_SHARES = ((0, 128), (128, 192))
 VECTOR_SHARE = (192, 544)
 SCALAR_SHARES = ((544, 640), (640, 768))
 HALVES = ((0, 192), (192, 384))
+FUSED = 64
 
 
 def tile_picked_sub_lin_none_sub_e_kernel(tc, xT, w_words, w_scales, gate, offs, pos1, pos2, out):
@@ -140,10 +141,13 @@ def tile_picked_sub_lin_none_sub_e_kernel(tc, xT, w_words, w_scales, gate, offs,
             nc.scalar.copy(y[:, columns(piece)], acc[:])
 
         nc.vector.tensor_tensor(term1[:], y[:].indirect(pos1_t[:]), gate1[:], MULT)
+        nc.vector.tensor_tensor(term2[:, :FUSED], y[:].indirect(pos2_t[:, : FUSED // STRIPE]), gate2[0][:, :FUSED], MULT)
         for a, b in HALVES:
+            a = max(a, FUSED)
             nc.scalar.activation(picked2[:, a:b], y[:].indirect(pos2_t[:, a // STRIPE : b // STRIPE]), COPY)
         for (a, b), weights in zip(HALVES, gate2):
-            nc.vector.tensor_tensor(term2[:, a:b], picked2[:, a:b], weights[:], MULT)
+            c = max(a, FUSED)
+            nc.vector.tensor_tensor(term2[:, c:b], picked2[:, c:b], weights[:, c - a :], MULT)
         for a, b in HALVES:
             nc.vector.tensor_tensor(total[:, a:b], term1[:, a:b], term2[:, a:b], ADD)
         nc.sync.dma_start(out=out, in_=total[:])

@@ -43,9 +43,8 @@ def tile_picked_sub_lin_none_sub_e_kernel(tc, xT, w_words, w_scales, gate, offs,
         w_plane = keep.tile([P, N], U8, name="w_plane", align_bytes=64)
         gate1 = keep.tile([P, V], F32, name="gate1")
         gate2 = [keep.tile([P, b - a], F32, name=f"gate2_{a}") for a, b in HALVES]
-        low_row = keep.tile([P, S], I32, name="low_row", align_bytes=64)
-        low_words = low_row[:].bitcast(U32)
-        low_pairs = low_row[:].bitcast(BF16).rearrange("p (n e) -> p n e", e=2)
+        outer = ((0, VECTOR_SHARE[0]), (VECTOR_SHARE[1], S))
+        low = {a: keep.tile([P, 2 * (b - a)], BF16, name=f"low{a}", align_bytes=64) for a, b in outer}
         shares = GPSIMD_SHARES + SCALAR_SHARES
         high = {
             a: keep.tile([P, 2 * (b - a)], BF16, name=f"high{a}", tag="turn" if a == 0 else f"high{a}", align_bytes=64)
@@ -53,7 +52,6 @@ def tile_picked_sub_lin_none_sub_e_kernel(tc, xT, w_words, w_scales, gate, offs,
         }
         row = keep.tile([P, S * PACK], BF16, name="row", align_bytes=64)
         groups = row[:].rearrange("p (n t) -> p n t", t=PACK)
-        group_words = row[:].bitcast(U32).rearrange("p (n u) -> p n u", u=2)
         codes = keep.tile([P, S], U32, name="codes", align_bytes=64)
         scales = keep.tile([P, S], U8, name="scales", align_bytes=64)
         term1 = keep.tile([P, V], F32, name="term1")
@@ -110,17 +108,18 @@ def tile_picked_sub_lin_none_sub_e_kernel(tc, xT, w_words, w_scales, gate, offs,
             )
             return acc
 
-        for t in range(2):
-            nc.vector.tensor_copy(low_pairs[:, :, t], x[t][:].indirect(offs_t[:]))
         a, b = VECTOR_SHARE
-        nc.scalar.copy(group_words[:, a:b, 0], low_words[:, a:b])
-        nc.gpsimd.tensor_copy(group_words[:, :a, 0], low_words[:, :a])
-        nc.gpsimd.tensor_copy(group_words[:, b:, 0], low_words[:, b:])
-
-        nc.vector.tensor_copy(groups[:, a:b, 2], x[2][:].indirect(entries(VECTOR_SHARE)))
-        for share in SCALAR_SHARES:
-            nc.vector.tensor_copy(high_row(share, 2), x[2][:].indirect(entries(share)))
-        for share in GPSIMD_SHARES:
+        for t in range(3):
+            nc.vector.tensor_copy(groups[:, a:b, t], x[t][:].indirect(entries(VECTOR_SHARE)))
+        for t in range(2):
+            for share in outer:
+                n = share[1] - share[0]
+                nc.scalar.activation(low[share[0]][:, t * n : (t + 1) * n], x[t][:].indirect(entries(share)), COPY)
+        for share in outer:
+            nc.gpsimd.tensor_copy(
+                groups[:, share[0] : share[1], :2], low[share[0]][:].rearrange("p (t n) -> p n t", t=2)
+            )
+        for share in shares:
             nc.scalar.activation(high_row(share, 2), x[2][:].indirect(entries(share)), COPY)
 
         nc.vector.tensor_copy(groups[:, a:b, 3], x[3][:].indirect(entries(VECTOR_SHARE)))

@@ -63,13 +63,14 @@ def tile_picked_sub_lin_none_sub_e_kernel(tc, xT, w_words, w_scales, gate, offs,
         nc.vector.memset(w_plane[:].bitcast(I32), 0)
         nc.sync.dma_start(out=x[0][:], in_=planes[:, 0, :])
         nc.sync.dma_start(offs_t[:], offs)
-        for t in (1, 2, 3):
+        for t in (1, 2):
             nc.sync.dma_start(out=x[t][:], in_=planes[:, t, :])
         for q in range(4):
             nc.sync.dma_start(
                 out=w_plane[QUADRANT * q : QUADRANT * q + 4, :].bitcast(I32),
                 in_=w_scales[0, 4 * q : 4 * q + 4, :].bitcast(I32),
             )
+        nc.sync.dma_start(out=x[3][:], in_=planes[:, 3, :])
         nc.sync.dma_start(out=w_codes[:], in_=w_words[0].rearrange("p n t -> p (n t)").bitcast(I32))
         nc.sync.dma_start(out=gate1[:], in_=gate[0])
         nc.sync.dma_start(out=gate2[0][:], in_=gate[1, :, HALVES[0][0] : HALVES[0][1]])

@@ -21,7 +21,8 @@ PACK = 4
 STRIPE = 16
 QUADRANT = 32
 PIECE = 128
-GPSIMD_SHARES = ((0, 128), (128, 192))
+GPSIMD_SHARES = ((0, 128),)
+HANDED = (128, 192)
 VECTOR_SHARE = (192, 544)
 SCALAR_SHARES = ((544, 640), (640, 768))
 HALVES = ((0, 192), (192, 384))
@@ -43,7 +44,8 @@ def tile_picked_sub_lin_none_sub_e_kernel(tc, xT, w_words, w_scales, gate, offs,
         w_plane = keep.tile([P, N], U8, name="w_plane", align_bytes=64)
         gate1 = keep.tile([P, V], F32, name="gate1")
         gate2 = [keep.tile([P, b - a], F32, name=f"gate2_{a}") for a, b in HALVES]
-        outer = ((0, VECTOR_SHARE[0]), (VECTOR_SHARE[1], S))
+        outer = ((0, HANDED[0]), (VECTOR_SHARE[1], S))
+        handed = keep.tile([P, HANDED[1] - HANDED[0]], BF16, name="handed", align_bytes=64)
         low = {a: keep.tile([P, 2 * (b - a)], BF16, name=f"low{a}", align_bytes=64) for a, b in outer}
         shares = GPSIMD_SHARES + SCALAR_SHARES
         high = {
@@ -111,7 +113,7 @@ def tile_picked_sub_lin_none_sub_e_kernel(tc, xT, w_words, w_scales, gate, offs,
 
         a, b = VECTOR_SHARE
         for t in range(3):
-            nc.vector.tensor_copy(groups[:, a:b, t], x[t][:].indirect(entries(VECTOR_SHARE)))
+            nc.vector.tensor_copy(groups[:, HANDED[0] : b, t], x[t][:].indirect(entries((HANDED[0], b))))
         for t in range(2):
             for share in outer:
                 n = share[1] - share[0]
@@ -124,17 +126,21 @@ def tile_picked_sub_lin_none_sub_e_kernel(tc, xT, w_words, w_scales, gate, offs,
             nc.scalar.activation(high_row(share, 2), x[2][:].indirect(entries(share)), COPY)
 
         nc.vector.tensor_copy(groups[:, a:b, 3], x[3][:].indirect(entries(VECTOR_SHARE)))
-        for share in shares:
+        for share in GPSIMD_SHARES:
             nc.scalar.activation(high_row(share, 3), x[3][:].indirect(entries(share)), COPY)
+        nc.scalar.activation(handed[:], x[3][:].indirect(entries(HANDED)), COPY)
+        for share in SCALAR_SHARES:
+            nc.scalar.activation(high_row(share, 3), x[3][:].indirect(entries(share)), COPY)
+        nc.vector.tensor_copy(groups[:, HANDED[0] : HANDED[1], 3], handed[:])
         for share in GPSIMD_SHARES:
             place(nc.gpsimd.tensor_copy, share)
         for share in SCALAR_SHARES:
             place(nc.scalar.copy, share)
 
-        middle_codes = keep.tile([P, 2 * PIECE], U32, name="middle_codes", tag="turn", align_bytes=64)
+        middle_codes = keep.tile([P, 3 * PIECE], U32, name="middle_codes", tag="turn", align_bytes=64)
         products = {}
         for piece in (0, 2, 3, 1, 4, 5):
-            words = middle_codes[:, columns(piece - 2)] if piece in (2, 3) else codes[:, columns(piece)]
+            words = middle_codes[:, columns(piece - 1)] if piece in (1, 2, 3) else codes[:, columns(piece)]
             products[piece] = multiply(piece, words)
         y = keep.tile([P, S], F32, name="y", align_bytes=64)
         for piece, acc in products.items():

@@ -21,10 +21,8 @@ PACK = 4
 STRIPE = 16
 QUADRANT = 32
 PIECE = 128
-GPSIMD_SHARES = ((0, 128),)
-HANDED = (128, 192)
-VECTOR_SHARE = (192, 544)
-SCALAR_SHARES = ((544, 640), (640, 768))
+SCALAR_SHARE = (0, 448)
+VECTOR_SHARE = (448, 768)
 HALVES = ((0, 192), (192, 384))
 FUSED = 64
 
@@ -44,18 +42,11 @@ def tile_picked_sub_lin_none_sub_e_kernel(tc, xT, w_words, w_scales, gate, offs,
         w_plane = keep.tile([P, N], U8, name="w_plane", align_bytes=64)
         gate1 = keep.tile([P, V], F32, name="gate1")
         gate2 = [keep.tile([P, b - a], F32, name=f"gate2_{a}") for a, b in HALVES]
-        outer = ((0, HANDED[0]), (VECTOR_SHARE[1], S))
-        handed = keep.tile([P, HANDED[1] - HANDED[0]], BF16, name="handed", align_bytes=64)
-        low = {a: keep.tile([P, 2 * (b - a)], BF16, name=f"low{a}", align_bytes=64) for a, b in outer}
-        shares = GPSIMD_SHARES + SCALAR_SHARES
-        high = {
-            a: keep.tile([P, 2 * (b - a)], BF16, name=f"high{a}", tag="turn" if a == 0 else f"high{a}", align_bytes=64)
-            for a, b in shares
-        }
         row = keep.tile([P, S * PACK], BF16, name="row", align_bytes=64)
         groups = row[:].rearrange("p (n t) -> p n t", t=PACK)
         codes = keep.tile([P, S], U32, name="codes", align_bytes=64)
         scales = keep.tile([P, S], U8, name="scales", align_bytes=64)
+        y = keep.tile([P, S], F32, name="y", align_bytes=64)
         term1 = keep.tile([P, V], F32, name="term1")
         picked2 = keep.tile([P, V], F32, name="picked2")
         term2 = keep.tile([P, V], F32, name="term2")
@@ -80,22 +71,26 @@ def tile_picked_sub_lin_none_sub_e_kernel(tc, xT, w_words, w_scales, gate, offs,
         nc.sync.dma_start(pos2_t[:], pos2)
         nc.sync.dma_start(out=gate2[1][:], in_=gate[1, :, HALVES[1][0] : HALVES[1][1]])
 
-        def entries(share):
-            return offs_t[:, share[0] // STRIPE : share[1] // STRIPE]
+        def picked(t, a, b):
+            return x[t][:].indirect(offs_t[:, a // STRIPE : b // STRIPE])
 
         def columns(piece):
             return slice(piece * PIECE, (piece + 1) * PIECE)
 
-        def high_row(share, t):
-            n = share[1] - share[0]
-            return high[share[0]][:, (t - 2) * n : (t - 1) * n]
+        for t in range(PACK):
+            a, b = VECTOR_SHARE
+            nc.vector.tensor_copy(groups[:, a:b, t], picked(t, a, b))
+            a, b = SCALAR_SHARE
+            step = PIECE if t == PACK - 1 else b - a
+            for c in range(a, b, step):
+                d = min(c + step, b)
+                nc.scalar.activation(groups[:, c:d, t], picked(t, c, d), COPY)
 
-        def place(copy, share):
-            copy(groups[:, share[0] : share[1], 2:], high[share[0]][:].rearrange("p (t n) -> p n t", t=2))
-
-        def multiply(piece, words):
+        products = {}
+        for piece in (0, 1, 4, 5, 2, 3):
+            words = codes[:, columns(piece)].bitcast(FP8X4)
             nc.vector.quantize_mx(
-                out=words.bitcast(FP8X4),
+                out=words,
                 scales=scales[:, columns(piece)],
                 in_=row[:, piece * PIECE * PACK : (piece + 1) * PIECE * PACK],
             )
@@ -104,45 +99,12 @@ def tile_picked_sub_lin_none_sub_e_kernel(tc, xT, w_words, w_scales, gate, offs,
                 out=acc[:],
                 lhsT=w_codes[:].bitcast(FP8X4),
                 lhsT_scale=w_plane[:],
-                rhs=words.bitcast(FP8X4),
+                rhs=words,
                 rhs_scale=scales[:, columns(piece)],
                 start=True,
                 stop=True,
             )
-            return acc
-
-        a, b = VECTOR_SHARE
-        for t in range(3):
-            nc.vector.tensor_copy(groups[:, HANDED[0] : b, t], x[t][:].indirect(entries((HANDED[0], b))))
-        for t in range(2):
-            for share in outer:
-                n = share[1] - share[0]
-                nc.scalar.activation(low[share[0]][:, t * n : (t + 1) * n], x[t][:].indirect(entries(share)), COPY)
-        for share in outer:
-            nc.gpsimd.tensor_copy(
-                groups[:, share[0] : share[1], :2], low[share[0]][:].rearrange("p (t n) -> p n t", t=2)
-            )
-        for share in shares:
-            nc.scalar.activation(high_row(share, 2), x[2][:].indirect(entries(share)), COPY)
-
-        nc.vector.tensor_copy(groups[:, a:b, 3], x[3][:].indirect(entries(VECTOR_SHARE)))
-        for share in GPSIMD_SHARES:
-            nc.scalar.activation(high_row(share, 3), x[3][:].indirect(entries(share)), COPY)
-        nc.scalar.activation(handed[:], x[3][:].indirect(entries(HANDED)), COPY)
-        for share in SCALAR_SHARES:
-            nc.scalar.activation(high_row(share, 3), x[3][:].indirect(entries(share)), COPY)
-        nc.vector.tensor_copy(groups[:, HANDED[0] : HANDED[1], 3], handed[:])
-        for share in GPSIMD_SHARES:
-            place(nc.gpsimd.tensor_copy, share)
-        for share in SCALAR_SHARES:
-            place(nc.scalar.copy, share)
-
-        middle_codes = keep.tile([P, 3 * PIECE], U32, name="middle_codes", tag="turn", align_bytes=64)
-        products = {}
-        for piece in (0, 2, 3, 1, 4, 5):
-            words = middle_codes[:, columns(piece - 1)] if piece in (1, 2, 3) else codes[:, columns(piece)]
-            products[piece] = multiply(piece, words)
-        y = keep.tile([P, S], F32, name="y", align_bytes=64)
+            products[piece] = acc
         for piece, acc in products.items():
             nc.scalar.copy(y[:, columns(piece)], acc[:])
 

@@ -106,7 +106,7 @@ def tile_picked_sub_lin_none_sub_e_kernel(tc, xT, w_words, w_scales, gate, offs,
             )
             products[piece] = acc
         for piece, acc in products.items():
-            nc.scalar.copy(y[:, columns(piece)], acc[:])
+            nc.vector.tensor_copy(y[:, columns(piece)], acc[:])
 
         nc.vector.tensor_tensor(term1[:], y[:].indirect(pos1_t[:]), gate1[:], MULT)
         nc.vector.tensor_tensor(term2[:, :FUSED], y[:].indirect(pos2_t[:, : FUSED // STRIPE]), gate2[0][:, :FUSED], MULT)

@@ -24,7 +24,7 @@ PIECE = 128
 SCALAR_SHARE = (0, 448)
 VECTOR_SHARE = (448, 768)
 HALVES = ((0, 192), (192, 384))
-FUSED = 64
+FETCHED = ((0, 192), (192, 320), (320, 384))
 
 
 def tile_picked_sub_lin_none_sub_e_kernel(tc, xT, w_words, w_scales, gate, offs, pos1, pos2, out):
@@ -109,13 +109,12 @@ def tile_picked_sub_lin_none_sub_e_kernel(tc, xT, w_words, w_scales, gate, offs,
             nc.vector.tensor_copy(y[:, columns(piece)], acc[:])
 
         nc.vector.tensor_tensor(term1[:], y[:].indirect(pos1_t[:]), gate1[:], MULT)
-        nc.vector.tensor_tensor(term2[:, :FUSED], y[:].indirect(pos2_t[:, : FUSED // STRIPE]), gate2[0][:, :FUSED], MULT)
-        for a, b in HALVES:
-            a = max(a, FUSED)
+        for a, b in FETCHED:
             nc.scalar.activation(picked2[:, a:b], y[:].indirect(pos2_t[:, a // STRIPE : b // STRIPE]), COPY)
-        for (a, b), weights in zip(HALVES, gate2):
-            c = max(a, FUSED)
-            nc.vector.tensor_tensor(term2[:, c:b], picked2[:, c:b], weights[:, c - a :], MULT)
-        for a, b in HALVES:
+        for a, b in FETCHED:
+            half = a // HALVES[1][0]
+            first = HALVES[half][0]
+            nc.vector.tensor_tensor(term2[:, a:b], picked2[:, a:b], gate2[half][:, a - first : b - first], MULT)
+        for a, b in FETCHED:
             nc.vector.tensor_tensor(total[:, a:b], term1[:, a:b], term2[:, a:b], ADD)
         nc.sync.dma_start(out=out, in_=total[:])

from contextlib import ExitStack

import concourse.mybir as mybir

K, T, D, S, V, N = 512, 2048, 2, 768, 384, 128
FLOPS = 2 * K * N * S

F32 = mybir.dt.float32
BF16 = mybir.dt.bfloat16
I32 = mybir.dt.int32
U32 = mybir.dt.uint32
U16 = mybir.dt.uint16
U8 = mybir.dt.uint8
FP8X4 = mybir.dt.float8_e4m3fn_x4
MULT = mybir.AluOpType.mult
ADD = mybir.AluOpType.add
COPY = mybir.ActivationFunctionType.Copy

P = 128
PACK = 4
STRIPE = 16
QUADRANT = 32
PIECE = 128
SCALAR_SHARE = (0, 448)
VECTOR_SHARE = (448, 768)
HALVES = ((0, 192), (192, 384))
FETCHED = ((0, 192), (192, 320), (320, 384))


def tile_picked_sub_lin_none_sub_e_kernel(tc, xT, w_words, w_scales, gate, offs, pos1, pos2, out):
    nc = tc.nc
    with ExitStack() as ctx:
        lists = ctx.enter_context(tc.tile_pool(name="lists", bufs=1))
        keep = ctx.enter_context(tc.tile_pool(name="keep", bufs=1))
        psum = ctx.enter_context(tc.psum_pool(name="psum", bufs=1))

        offs_t = lists.tile([P, S // STRIPE], U16, name="offs_t")
        pos1_t = lists.tile([P, V // STRIPE], U16, name="pos1_t")
        pos2_t = lists.tile([P, V // STRIPE], U16, name="pos2_t")
        x = [keep.tile([P, T], F32, name=f"x{t}", align_bytes=256) for t in range(PACK)]
        w_codes = keep.tile([P, N], I32, name="w_codes", align_bytes=64)
        w_plane = keep.tile([P, N], U8, name="w_plane", align_bytes=64)
        gate1 = keep.tile([P, V], F32, name="gate1")
        gate2 = [keep.tile([P, b - a], F32, name=f"gate2_{a}") for a, b in HALVES]
        row = keep.tile([P, S * PACK], BF16, name="row", align_bytes=64)
        groups = row[:].rearrange("p (n t) -> p n t", t=PACK)
        codes = keep.tile([P, S], U32, name="codes", align_bytes=64)
        scales = keep.tile([P, S], U8, name="scales", align_bytes=64)
        y = keep.tile([P, S], F32, name="y", align_bytes=64)
        term1 = keep.tile([P, V], F32, name="term1")
        picked2 = keep.tile([P, V], F32, name="picked2")
        term2 = keep.tile([P, V], F32, name="term2")
        total = keep.tile([P, V], F32, name="total", align_bytes=256)

        planes = xT.rearrange("(p t) n -> p t n", t=PACK)
        nc.vector.memset(w_plane[:].bitcast(I32), 0)
        nc.sync.dma_start(out=x[0][:], in_=planes[:, 0, :])
        nc.sync.dma_start(offs_t[:], offs)
        for t in (1, 2):
            nc.sync.dma_start(out=x[t][:], in_=planes[:, t, :])
        for q in range(4):
            nc.sync.dma_start(
                out=w_plane[QUADRANT * q : QUADRANT * q + 4, :].bitcast(I32),
                in_=w_scales[0, 4 * q : 4 * q + 4, :].bitcast(I32),
            )
        nc.sync.dma_start(out=x[3][:], in_=planes[:, 3, :])
        nc.sync.dma_start(out=w_codes[:], in_=w_words[0].rearrange("p n t -> p (n t)").bitcast(I32))
        nc.sync.dma_start(out=gate1[:], in_=gate[0])
        nc.sync.dma_start(out=gate2[0][:], in_=gate[1, :, HALVES[0][0] : HALVES[0][1]])
        nc.sync.dma_start(pos1_t[:], pos1)
        nc.sync.dma_start(pos2_t[:], pos2)
        nc.sync.dma_start(out=gate2[1][:], in_=gate[1, :, HALVES[1][0] : HALVES[1][1]])

        def picked(t, a, b):
            return x[t][:].indirect(offs_t[:, a // STRIPE : b // STRIPE])

        def columns(piece):
            return slice(piece * PIECE, (piece + 1) * PIECE)

        for t in range(PACK):
            a, b = VECTOR_SHARE
            nc.vector.tensor_copy(groups[:, a:b, t], picked(t, a, b))
            a, b = SCALAR_SHARE
            step = PIECE if t == PACK - 1 else b - a
            for c in range(a, b, step):
                d = min(c + step, b)
                nc.scalar.activation(groups[:, c:d, t], picked(t, c, d), COPY)

        products = {}
        for piece in (0, 1, 4, 5, 2, 3):
            words = codes[:, columns(piece)].bitcast(FP8X4)
            nc.vector.quantize_mx(
                out=words,
                scales=scales[:, columns(piece)],
                in_=row[:, piece * PIECE * PACK : (piece + 1) * PIECE * PACK],
            )
            acc = psum.tile([P, PIECE], F32, name=f"acc{piece}")
            nc.tensor.matmul_mx(
                out=acc[:],
                lhsT=w_codes[:].bitcast(FP8X4),
                lhsT_scale=w_plane[:],
                rhs=words,
                rhs_scale=scales[:, columns(piece)],
                start=True,
                stop=True,
            )
            products[piece] = acc
        for piece, acc in products.items():
            nc.vector.tensor_copy(y[:, columns(piece)], acc[:])

        nc.vector.tensor_tensor(term1[:], y[:].indirect(pos1_t[:]), gate1[:], MULT)
        for a, b in FETCHED:
            nc.scalar.activation(picked2[:, a:b], y[:].indirect(pos2_t[:, a // STRIPE : b // STRIPE]), COPY)
        for a, b in FETCHED:
            half = a // HALVES[1][0]
            first = HALVES[half][0]
            nc.vector.tensor_tensor(term2[:, a:b], picked2[:, a:b], gate2[half][:, a - first : b - first], MULT)
        for a, b in FETCHED:
            nc.vector.tensor_tensor(total[:, a:b], term1[:, a:b], term2[:, a:b], ADD)
        nc.sync.dma_start(out=out, in_=total[:])
